import numpy as np
import ml_dtypes


def mxq(x, axis, fmt="e4m3"):
    dtype, down = {"e4m3": (ml_dtypes.float8_e4m3fn, 7), "e5m2": (ml_dtypes.float8_e5m2, 14)}[fmt]
    v = np.moveaxis(np.asarray(x, np.float32).astype(ml_dtypes.bfloat16).astype(np.float64), axis, -1)
    blocks = v.reshape(v.shape[:-1] + (-1, 32))
    amax = np.abs(blocks).max(-1, keepdims=True)
    byte = np.maximum(np.where(amax > 0, np.frexp(amax)[1] - 1 + 127, 0) - down, 1)
    scale = np.exp2(byte - 127.0)
    codes = (blocks / scale).astype(np.float32).astype(dtype).astype(np.float64)
    return np.moveaxis((codes * scale).reshape(v.shape), -1, axis)


WIDE = False


def mx_kscale(k):
    if not WIDE:
        return np.ones(k)
    levels = np.array([10, -10, 5, -5, 0])
    if k % 512:
        return np.exp2(np.random.permutation(np.resize(levels, k // 32))).repeat(32)
    a = np.empty((k // 512, 16))
    for p in range(k // 512):
        a[p, :8] = np.random.permutation(np.resize(levels, 8))
        for g in range(8):
            far = levels[np.abs(levels - a[p, g]) >= 10]
            a[p, g + 8] = far[np.random.randint(len(far))]
    return np.exp2(a.ravel()).repeat(32)


def f64(x):
    return np.asarray(x).astype(np.float64)


def striped(idx):
    return np.tile(idx.reshape(-1, 16).T, (8, 1)).astype(np.uint16)


def unstriped(offs):
    return offs[:16].T.reshape(-1).astype(np.int64)


def pack_weight(w):
    k, n = w.shape
    w = f64(np.asarray(w, np.float32).astype(ml_dtypes.bfloat16)).reshape(k // 32, 32, n)
    amax = np.abs(w).max(1)
    byte = np.clip(np.where(amax > 0, np.frexp(amax)[1] - 1 + 127 - 7, 1), 1, 254)
    scaled = (w * np.exp2(127.0 - byte)[:, None, :]).reshape(k, n).astype(np.float32)
    words = np.ascontiguousarray(scaled.reshape(k // 512, 128, 4, n).transpose(0, 1, 3, 2)).astype(ml_dtypes.float8_e4m3fn).view(np.uint8)
    return words, np.ascontiguousarray(byte.astype(np.uint8).reshape(k // 512, 16, n))


def unpack_weight(words, scales):
    g, p, n, _ = words.shape
    vals = np.ascontiguousarray(words).view(ml_dtypes.float8_e4m3fn).astype(np.float64) * np.repeat(np.exp2(scales.astype(np.float64) - 127.0), 8, axis=1)[..., None]
    return vals.transpose(0, 1, 3, 2).reshape(g * 512, n)


def planes(y):
    n, m = y.shape
    v = y.astype(np.float32).astype(ml_dtypes.bfloat16).astype(np.float64).reshape(n // 32, 32, m)
    top = np.abs(v).max(1)
    byte = np.clip(np.where(top > 0, np.frexp(top)[1] - 1 + 127 - 7, 1), 1, 254)
    codes = (v * np.exp2(127.0 - byte)[:, None, :]).reshape(n, m).astype(np.float32).astype(ml_dtypes.float8_e4m3fn).view(np.uint8)
    words = codes.reshape(n // 512, 128, 4, m).transpose(0, 1, 3, 2)
    return np.ascontiguousarray(words), np.ascontiguousarray(byte.astype(np.uint8).reshape(n // 512, 16, m))


def relu(v):
    return np.maximum(v, 0.0)


K, T, S, H, N = 512, 4096, 1024, 512, 512
P = 2 ** 7


def setup_inputs():
    n = np.random.standard_normal
    s = mx_kscale(K)[:, None]
    u = mx_kscale(H)
    packed_xT = pack_weight(n((K, T)) * s)
    return {
        "x_words": packed_xT[0],
        "x_scales": packed_xT[1],
        "w1": (n((K, H)) / np.sqrt(K) / s * u).astype(np.float32),
        "w2": (n((H, N)) / np.sqrt(H) / u[:, None]).astype(np.float32),
        "score": (np.tile(n(T), (P, 1))).astype(np.float32),
        "offs": striped(np.random.permutation(T)[:S]),
    }


def reference(x_words, x_scales, w1, w2, score, offs):
    xq = unpack_weight(x_words, x_scales)[:, unstriped(offs)]
    y = mxq(f64(w1), 0, "e4m3").T @ xq
    sc = f64(score)[:1][:, unstriped(offs)]
    ee = np.exp(sc)
    p = y * ee
    total = ee.sum(axis=1, keepdims=True)
    ctx = p.sum(axis=1, keepdims=True) / total
    z = relu(y + ctx)
    out_0 = mxq(f64(w2), 0, "e4m3").T @ mxq(z, 0, "e4m3")
    return (out_0,) + planes(out_0)

@@ -1,0 +1,228 @@
+from contextlib import ExitStack
+
+import concourse.mybir as mybir
+from concourse.masks import make_identity
+
+K, T, S, H, N = 512, 4096, 1024, 512, 512
+FLOPS = 2 * K * H * S + 2 * H * N * S
+
+F32 = mybir.dt.float32
+BF16 = mybir.dt.bfloat16
+I32 = mybir.dt.int32
+U32 = mybir.dt.uint32
+U16 = mybir.dt.uint16
+U8 = mybir.dt.uint8
+FP8X4 = mybir.dt.float8_e4m3fn_x4
+ALU = mybir.AluOpType
+ACT = mybir.ActivationFunctionType
+AXIS = mybir.AxisListType
+
+P = 128
+PACK = 4
+BANK = 512
+HALVES = S // BANK
+WIDTHS = (128, 256, 256, 256, 128)
+STARTS = tuple(sum(WIDTHS[:c]) for c in range(len(WIDTHS)))
+CHUNKS = len(WIDTHS)
+QUADS = 4
+RUN = 4
+LOADED = BANK
+SPREAD = (T - LOADED) // P
+
+
+def interleave(engine_copy, out, planes):
+    engine_copy(
+        out=out.rearrange("p (c i) t -> p c t i", i=RUN),
+        in_=planes.rearrange("p t (c i) -> p c t i", i=RUN),
+    )
+
+
+def tile_picked_ygcb_relu_po_kernel(tc, x_words, x_scales, w1, w2, score, offs, out_0, out_1, out_2):
+    nc = tc.nc
+    with ExitStack() as ctx:
+        keep = ctx.enter_context(tc.tile_pool(name="keep", bufs=1))
+        psum = ctx.enter_context(tc.psum_pool(name="psum", bufs=1))
+
+        def bank(b):
+            return psum.tile([P, BANK], F32, name="bank%d" % b)
+
+        offsets = keep.tile([P, S // 16], U16, name="offsets")
+        nc.sync.dma_start(offsets[:], offs)
+        score_cols = keep.tile([P, SPREAD], F32, name="score_cols")
+        nc.sync.dma_start(out=score_cols[:], in_=score[0, LOADED:].rearrange("(p c) -> p c", p=P))
+
+        scale_table = keep.tile([P, T], U8, name="scale_table", tag="scales_then_picked", align_bytes=64)
+        nc.gpsimd.memset(scale_table[:, : T // 2].bitcast(I32), 0)
+        nc.vector.memset(scale_table[:, T // 2 :].bitcast(I32), 0)
+        for q in range(QUADS):
+            queue = nc.sync if q % 2 == 0 else nc.scalar
+            queue.dma_start(
+                out=scale_table[32 * q : 32 * q + 4, :].bitcast(I32),
+                in_=x_scales[0, 4 * q : 4 * q + 4, :].bitcast(I32),
+            )
+
+        score_table = keep.tile([P, T], F32, name="score_table")
+        nc.sync.dma_start(out=score_table[:, :LOADED], in_=score[:, :LOADED])
+        w1_raw = keep.tile([P, PACK, H], F32, name="w1_raw", tag="w1_then_weights")
+        nc.sync.dma_start(out=w1_raw[:], in_=w1.rearrange("(p j) c -> p j c", j=PACK))
+        word_table = keep.tile([P, T], I32, name="word_table", align_bytes=64)
+        nc.sync.dma_start(out=word_table[:], in_=x_words[0].rearrange("p c r -> p (c r)").bitcast(I32))
+        w2_raw = keep.tile([P, PACK, N], F32, name="w2_raw", tag="w2_then_z")
+        nc.sync.dma_start(out=w2_raw[:], in_=w2.rearrange("(p j) c -> p j c", j=PACK))
+
+        ident = keep.tile([P, P], F32, name="ident")
+        make_identity(nc, ident[:])
+
+
+        table_view = score_table[:, LOADED:].rearrange("p (n c) -> p n c", c=SPREAD)
+        for g in range(SPREAD // 4):
+            spread = bank(g)
+            for c in range(4):
+                col = 4 * g + c
+                nc.tensor.transpose(
+                    spread[:, P * c : P * (c + 1)],
+                    score_cols[:, col : col + 1].to_broadcast([P, P]),
+                    ident[:],
+                )
+            nc.scalar.copy(
+                out=table_view[:, :, 4 * g : 4 * g + 4],
+                in_=spread[:].rearrange("p (c n) -> p n c", c=4),
+            )
+
+        x_scale = keep.tile([P, S], U8, name="x_scale", align_bytes=64)
+        nc.vector.tensor_copy(x_scale[:], scale_table[:].indirect(offsets[:]))
+
+        picked = keep.tile([P, S], F32, name="picked", tag="scales_then_picked", align_bytes=64)
+        nc.vector.tensor_copy(picked[:], score_table[:].indirect(offsets[:]))
+        neg_max = keep.tile([P, 1], F32, name="neg_max")
+        nc.vector.tensor_reduce(out=neg_max[:], in_=picked[:], axis=AXIS.X, op=ALU.max, negate=True)
+
+        def quantize_weight(raw, label, tag):
+            grouped = keep.tile([P, PACK, P, PACK], BF16, name=label + "_grouped", tag=tag, align_bytes=64)
+            nc.scalar.copy(
+                out=grouped[:].rearrange("p t m j -> p m j t"),
+                in_=raw[:].rearrange("p j (m t) -> p m j t", t=PACK),
+            )
+            codes = keep.tile([P, PACK * P], U32, name=label + "_codes", align_bytes=64)
+            scales = keep.tile([P, PACK * P], U8, name=label + "_scales", align_bytes=64)
+            nc.vector.quantize_mx(
+                out=codes[:].bitcast(FP8X4), scales=scales[:], in_=grouped[:].rearrange("p t m j -> p (t m j)")
+            )
+            return codes, scales
+
+        w1_codes, w1_scales = quantize_weight(w1_raw, "w1", "w1_then_codes")
+
+        weights = keep.tile([P, S], F32, name="weights", tag="w1_then_weights")
+        total = keep.tile([P, 1], F32, name="total")
+        nc.scalar.activation(out=weights[:], in_=picked[:], func=ACT.Exp, bias=neg_max[:], scale=1.0, accum_out=total[:])
+
+        x_codes = keep.tile([P, S], U32, name="x_codes", tag="w1_then_codes", align_bytes=64)
+        for h in range(HALVES):
+            nc.vector.tensor_copy(
+                x_codes[:, BANK * h : BANK * (h + 1)],
+                word_table[:].bitcast(U32).indirect(offsets[:, h * (BANK // 16) : (h + 1) * (BANK // 16)]),
+            )
+
+        inv_total = keep.tile([P, 1], F32, name="inv_total")
+        nc.vector.reciprocal(inv_total[:], total[:])
+
+        y = {}
+        for t in range(PACK):
+            for h in range(HALVES):
+                y[t, h] = bank(HALVES * t + h)
+                nc.tensor.matmul_mx(
+                    out=y[t, h][:],
+                    lhsT=w1_codes[:, P * t : P * (t + 1)].bitcast(FP8X4),
+                    lhsT_scale=w1_scales[:, P * t : P * (t + 1)],
+                    rhs=x_codes[:, BANK * h : BANK * (h + 1)].bitcast(FP8X4),
+                    rhs_scale=x_scale[:, BANK * h : BANK * (h + 1)],
+                    start=True,
+                    stop=True,
+                )
+
+        w2_codes, w2_scales = quantize_weight(w2_raw, "w2", "w2_grouped")
+
+        z_planes = keep.tile([P, PACK, S], BF16, name="z_planes", tag="w2_then_z")
+        for t in range(PACK):
+            part = keep.tile([P, HALVES], F32, name="part%d" % t)
+            for h in range(HALVES):
+                weighted = keep.tile([P, BANK], BF16, name="weighted%d_%d" % (t, h))
+                nc.vector.scalar_tensor_tensor(
+                    out=weighted[:],
+                    in0=y[t, h][:],
+                    scalar=inv_total[:],
+                    in1=weights[:, BANK * h : BANK * (h + 1)],
+                    op0=ALU.mult,
+                    op1=ALU.mult,
+                    accum_out=part[:, h : h + 1],
+                )
+            context = keep.tile([P, 1], F32, name="context%d" % t)
+            nc.vector.tensor_tensor(out=context[:], in0=part[:, 0:1], in1=part[:, 1:2], op=ALU.add)
+            cuts = (0, WIDTHS[0], BANK, S) if t == PACK - 1 else (0, BANK, S)
+            for c0, c1 in zip(cuts, cuts[1:]):
+                h = c0 // BANK
+                nc.scalar.activation(
+                    out=z_planes[:, t, c0:c1],
+                    in_=y[t, h][:, c0 - BANK * h : c1 - BANK * h],
+                    func=ACT.Relu,
+                    bias=context[:],
+                    scale=1.0,
+                )
+
+        out_rows = out_0.rearrange("(p t) j -> p t j", t=PACK)
+        out_words = out_1[0].rearrange("p c r -> p (c r)").bitcast(I32)
+        out_codes = keep.tile([P, S], I32, name="out_codes", align_bytes=64)
+        out_scales = keep.tile([P, S], U8, name="out_scales", align_bytes=64)
+
+        def second_product(c):
+            width = WIDTHS[c]
+            cols = slice(STARTS[c], STARTS[c] + width)
+            z_grouped = keep.tile([P, width, PACK], BF16, name="z_grouped%d" % c, align_bytes=64)
+            interleave(nc.scalar.copy if c == CHUNKS - 1 else nc.vector.tensor_copy, z_grouped[:], z_planes[:, :, cols])
+            z_codes = keep.tile([P, width], U32, name="z_codes%d" % c, align_bytes=64)
+            z_scales = keep.tile([P, width], U8, name="z_scales%d" % c, align_bytes=64)
+            nc.vector.quantize_mx(
+                out=z_codes[:].bitcast(FP8X4), scales=z_scales[:], in_=z_grouped[:].rearrange("p c t -> p (c t)")
+            )
+            result = keep.tile([P, PACK, width], F32, name="result%d" % c)
+            per_bank = BANK // width
+            for t0 in range(0, PACK, per_bank):
+                acc = bank((PACK * STARTS[c] + t0 * width) // BANK)
+                for v in range(per_bank):
+                    t = t0 + v
+                    nc.tensor.matmul_mx(
+                        out=acc[:, width * v : width * (v + 1)],
+                        lhsT=w2_codes[:, P * t : P * (t + 1)].bitcast(FP8X4),
+                        lhsT_scale=w2_scales[:, P * t : P * (t + 1)],
+                        rhs=z_codes[:].bitcast(FP8X4),
+                        rhs_scale=z_scales[:],
+                        start=True,
+                        stop=True,
+                    )
+                nc.scalar.copy(out=result[:, t0 : t0 + per_bank, :].rearrange("p t c -> p (t c)"), in_=acc[:])
+            nc.sync.dma_start(out=out_rows[:, :, cols], in_=result[:])
+            return result
+
+        def hand_on(c, result):
+            width = WIDTHS[c]
+            cols = slice(STARTS[c], STARTS[c] + width)
+            grouped = keep.tile([P, width, PACK], BF16, name="out_grouped%d" % c, align_bytes=64)
+            interleave(nc.vector.tensor_copy, grouped[:], result[:])
+            nc.vector.quantize_mx(
+                out=out_codes[:, cols].bitcast(FP8X4),
+                scales=out_scales[:, cols],
+                in_=grouped[:].rearrange("p c t -> p (c t)"),
+            )
+
+        results = [second_product(c) for c in range(CHUNKS)]
+        for c in range(CHUNKS):
+            hand_on(c, results[c])
+        early = STARTS[3]
+        nc.sync.dma_start(out=out_words[:, :early], in_=out_codes[:, :early])
+        nc.sync.dma_start(out=out_words[:, early:], in_=out_codes[:, early:])
+        for q in range(QUADS):
+            queue = nc.sync if q % 2 == 0 else nc.scalar
+            queue.dma_start(
+                out=out_2[0, 4 * q : 4 * q + 4, :].bitcast(I32),
+                in_=out_scales[32 * q : 32 * q + 4, :].bitcast(I32),
+            )

@@ -48,7 +48,7 @@ def tile_picked_ygcb_relu_po_kernel(tc, x_words, x_scales, w1, w2, score, offs, 
 
         offsets = keep.tile([P, S // 16], U16, name="offsets")
         nc.sync.dma_start(offsets[:], offs)
-        score_cols = keep.tile([P, SPREAD], F32, name="score_cols")
+        score_cols = keep.tile([P, SPREAD], F32, name="score_cols", tag="w1_then_codes", align_bytes=64)
         nc.sync.dma_start(out=score_cols[:], in_=score[0, LOADED:].rearrange("(p c) -> p c", p=P))
 
         scale_table = keep.tile([P, T], U8, name="scale_table", tag="scales_then_picked", align_bytes=64)
@@ -74,6 +74,9 @@ def tile_picked_ygcb_relu_po_kernel(tc, x_words, x_scales, w1, w2, score, offs, 
         make_identity(nc, ident[:])
 
 
+        warm = keep.tile([P, 1], F32, name="warm")
+        nc.scalar.activation(out=warm[:], in_=ident[:, 0:1], func=ACT.Exp)
+
         table_view = score_table[:, LOADED:].rearrange("p (n c) -> p n c", c=SPREAD)
         for g in range(SPREAD // 4):
             spread = bank(g)
@@ -84,7 +87,8 @@ def tile_picked_ygcb_relu_po_kernel(tc, x_words, x_scales, w1, w2, score, offs, 
                     score_cols[:, col : col + 1].to_broadcast([P, P]),
                     ident[:],
                 )
-            nc.scalar.copy(
+            copy = nc.vector.tensor_copy if g == SPREAD // 4 - 1 else nc.scalar.copy
+            copy(
                 out=table_view[:, :, 4 * g : 4 * g + 4],
                 in_=spread[:].rearrange("p (c n) -> p n c", c=4),
             )
@@ -94,23 +98,30 @@ def tile_picked_ygcb_relu_po_kernel(tc, x_words, x_scales, w1, w2, score, offs, 
 
         picked = keep.tile([P, S], F32, name="picked", tag="scales_then_picked", align_bytes=64)
         nc.vector.tensor_copy(picked[:], score_table[:].indirect(offsets[:]))
+        half_max = keep.tile([P, HALVES], F32, name="half_max", tag="max_then_scales", align_bytes=64)
+        nc.vector.tensor_reduce(
+            out=half_max[:], in_=picked[:].rearrange("p (h c) -> p h c", h=HALVES), axis=AXIS.X, op=ALU.max
+        )
         neg_max = keep.tile([P, 1], F32, name="neg_max")
-        nc.vector.tensor_reduce(out=neg_max[:], in_=picked[:], axis=AXIS.X, op=ALU.max, negate=True)
+        nc.vector.tensor_reduce(out=neg_max[:], in_=half_max[:], axis=AXIS.X, op=ALU.max, negate=True)
 
-        def quantize_weight(raw, label, tag):
+        def group_weight(raw, label, tag):
             grouped = keep.tile([P, PACK, P, PACK], BF16, name=label + "_grouped", tag=tag, align_bytes=64)
             nc.scalar.copy(
                 out=grouped[:].rearrange("p t m j -> p m j t"),
                 in_=raw[:].rearrange("p j (m t) -> p m j t", t=PACK),
             )
+            return grouped
+
+        def quantize_weight(grouped, label, tag):
             codes = keep.tile([P, PACK * P], U32, name=label + "_codes", align_bytes=64)
-            scales = keep.tile([P, PACK * P], U8, name=label + "_scales", align_bytes=64)
+            scales = keep.tile([P, PACK * P], U8, name=label + "_scales", tag=tag, align_bytes=64)
             nc.vector.quantize_mx(
                 out=codes[:].bitcast(FP8X4), scales=scales[:], in_=grouped[:].rearrange("p t m j -> p (t m j)")
             )
             return codes, scales
 
-        w1_codes, w1_scales = quantize_weight(w1_raw, "w1", "w1_then_codes")
+        w1_codes, w1_scales = quantize_weight(group_weight(w1_raw, "w1", "w1_then_codes"), "w1", "max_then_scales")
 
         weights = keep.tile([P, S], F32, name="weights", tag="w1_then_weights")
         total = keep.tile([P, 1], F32, name="total")
@@ -140,11 +151,11 @@ def tile_picked_ygcb_relu_po_kernel(tc, x_words, x_scales, w1, w2, score, offs, 
                     stop=True,
                 )
 
-        w2_codes, w2_scales = quantize_weight(w2_raw, "w2", "w2_grouped")
+        w2_grouped = group_weight(w2_raw, "w2", "scales_then_picked")
 
         z_planes = keep.tile([P, PACK, S], BF16, name="z_planes", tag="w2_then_z")
         for t in range(PACK):
-            part = keep.tile([P, HALVES], F32, name="part%d" % t)
+            part = keep.tile([P, HALVES], F32, name="part%d" % t, align_bytes=64)
             for h in range(HALVES):
                 weighted = keep.tile([P, BANK], BF16, name="weighted%d_%d" % (t, h))
                 nc.vector.scalar_tensor_tensor(
@@ -168,6 +179,8 @@ def tile_picked_ygcb_relu_po_kernel(tc, x_words, x_scales, w1, w2, score, offs, 
                     bias=context[:],
                     scale=1.0,
                 )
+
+        w2_codes, w2_scales = quantize_weight(w2_grouped, "w2", "part1")
 
         out_rows = out_0.rearrange("(p t) j -> p t j", t=PACK)
         out_words = out_1[0].rearrange("p c r -> p (c r)").bitcast(I32)

@@ -26,8 +26,8 @@ STARTS = tuple(sum(WIDTHS[:c]) for c in range(len(WIDTHS)))
 CHUNKS = len(WIDTHS)
 QUADS = 4
 RUN = 4
-LOADED = BANK
-SPREAD = (T - LOADED) // P
+ROW = P - 1
+SCALAR_Z = 3
 
 
 def interleave(engine_copy, out, planes):
@@ -48,92 +48,111 @@ def tile_picked_ygcb_relu_po_kernel(tc, x_words, x_scales, w1, w2, score, offs, 
 
         offsets = keep.tile([P, S // 16], U16, name="offsets")
         nc.sync.dma_start(offsets[:], offs)
-        score_cols = keep.tile([P, SPREAD], F32, name="score_cols", tag="w1_then_codes", align_bytes=64)
-        nc.sync.dma_start(out=score_cols[:], in_=score[0, LOADED:].rearrange("(p c) -> p c", p=P))
 
-        scale_table = keep.tile([P, T], U8, name="scale_table", tag="scales_then_picked", align_bytes=64)
-        nc.gpsimd.memset(scale_table[:, : T // 2].bitcast(I32), 0)
-        nc.vector.memset(scale_table[:, T // 2 :].bitcast(I32), 0)
-        for q in range(QUADS):
-            queue = nc.sync if q % 2 == 0 else nc.scalar
-            queue.dma_start(
-                out=scale_table[32 * q : 32 * q + 4, :].bitcast(I32),
-                in_=x_scales[0, 4 * q : 4 * q + 4, :].bitcast(I32),
-            )
-
+        scale_table = keep.tile([P, T], U8, name="scale_table", tag="scales_then_w2", align_bytes=64)
+        nc.vector.memset(scale_table[:].bitcast(I32), 0)
         score_table = keep.tile([P, T], F32, name="score_table")
-        nc.sync.dma_start(out=score_table[:, :LOADED], in_=score[:, :LOADED])
-        w1_raw = keep.tile([P, PACK, H], F32, name="w1_raw", tag="w1_then_weights")
+        nc.vector.memset(score_table[:ROW, :].bitcast(I32), 0)
+        x_scale = keep.tile([P, S], U8, name="x_scale", align_bytes=64)
+        nc.vector.memset(x_scale[:].bitcast(I32), 0)
+
+        nc.sync.dma_start(out=score_table[ROW:, :], in_=score[0:1, :])
+        w1_raw = keep.tile([P, PACK, H], F32, name="w1_raw")
         nc.sync.dma_start(out=w1_raw[:], in_=w1.rearrange("(p j) c -> p j c", j=PACK))
+        nc.sync.dma_start(out=scale_table[0:P:8, :].bitcast(I32), in_=x_scales[0].bitcast(I32))
         word_table = keep.tile([P, T], I32, name="word_table", align_bytes=64)
         nc.sync.dma_start(out=word_table[:], in_=x_words[0].rearrange("p c r -> p (c r)").bitcast(I32))
-        w2_raw = keep.tile([P, PACK, N], F32, name="w2_raw", tag="w2_then_z")
-        nc.sync.dma_start(out=w2_raw[:], in_=w2.rearrange("(p j) c -> p j c", j=PACK))
+
+        def load_w2_half(u, tag):
+            raw = keep.tile([P, PACK, N // 2], F32, name="w2_raw%d" % u, tag=tag, align_bytes=64)
+            nc.sync.dma_start(out=raw[:], in_=w2.rearrange("(p j) c -> p j c", j=PACK)[:, :, u * (N // 2) : (u + 1) * (N // 2)])
+            return raw
+
+        w2_raw = [load_w2_half(0, "w2_first_half")]
 
         ident = keep.tile([P, P], F32, name="ident")
         make_identity(nc, ident[:])
 
-
         warm = keep.tile([P, 1], F32, name="warm")
         nc.scalar.activation(out=warm[:], in_=ident[:, 0:1], func=ACT.Exp)
 
-        table_view = score_table[:, LOADED:].rearrange("p (n c) -> p n c", c=SPREAD)
-        for g in range(SPREAD // 4):
-            spread = bank(g)
-            for c in range(4):
-                col = 4 * g + c
-                nc.tensor.transpose(
-                    spread[:, P * c : P * (c + 1)],
-                    score_cols[:, col : col + 1].to_broadcast([P, P]),
-                    ident[:],
-                )
-            copy = nc.vector.tensor_copy if g == SPREAD // 4 - 1 else nc.scalar.copy
-            copy(
-                out=table_view[:, :, 4 * g : 4 * g + 4],
-                in_=spread[:].rearrange("p (c n) -> p n c", c=4),
-            )
+        def half(h):
+            return slice(BANK * h, BANK * (h + 1))
 
-        x_scale = keep.tile([P, S], U8, name="x_scale", align_bytes=64)
-        nc.vector.tensor_copy(x_scale[:], scale_table[:].indirect(offsets[:]))
+        def half_list(h):
+            return offsets[:, h * (BANK // 16) : (h + 1) * (BANK // 16)]
 
-        picked = keep.tile([P, S], F32, name="picked", tag="scales_then_picked", align_bytes=64)
-        nc.vector.tensor_copy(picked[:], score_table[:].indirect(offsets[:]))
-        half_max = keep.tile([P, HALVES], F32, name="half_max", tag="max_then_scales", align_bytes=64)
-        nc.vector.tensor_reduce(
-            out=half_max[:], in_=picked[:].rearrange("p (h c) -> p h c", h=HALVES), axis=AXIS.X, op=ALU.max
+        w1_grouped = keep.tile([P, PACK, P, PACK], BF16, name="w1_grouped", align_bytes=64)
+        nc.scalar.copy(
+            out=w1_grouped[:].rearrange("p t m j -> p m j t"), in_=w1_raw[:].rearrange("p j (m t) -> p m j t", t=PACK)
         )
-        neg_max = keep.tile([P, 1], F32, name="neg_max")
-        nc.vector.tensor_reduce(out=neg_max[:], in_=half_max[:], axis=AXIS.X, op=ALU.max, negate=True)
 
-        def group_weight(raw, label, tag):
-            grouped = keep.tile([P, PACK, P, PACK], BF16, name=label + "_grouped", tag=tag, align_bytes=64)
-            nc.scalar.copy(
-                out=grouped[:].rearrange("p t m j -> p m j t"),
-                in_=raw[:].rearrange("p j (m t) -> p m j t", t=PACK),
-            )
-            return grouped
+        picked = keep.tile([P, S], F32, name="picked")
+        for h in range(HALVES):
+            nc.vector.tensor_copy(picked[:, half(h)], score_table[:].indirect(half_list(h)))
+        cols = keep.tile([P, S // P], F32, name="cols")
+        for h in range(HALVES):
+            turned = bank(6 + h)
+            for c in range(4):
+                nc.tensor.transpose(turned[:, P * c : P * (c + 1)], picked[:, BANK * h + P * c : BANK * h + P * (c + 1)], ident[:])
+            nc.scalar.copy(out=cols[:, 4 * h : 4 * h + 4], in_=turned[:].rearrange("p (c n) -> p c n", c=4)[:, :, ROW])
 
-        def quantize_weight(grouped, label, tag):
+        picked_scale = keep.tile([P, S], U8, name="picked_scale", align_bytes=64)
+        nc.vector.tensor_copy(picked_scale[:, half(0)], scale_table[:].indirect(half_list(0)))
+        col_max = keep.tile([P, 1], F32, name="col_max", tag="max_then_codes", align_bytes=64)
+        nc.vector.tensor_reduce(out=col_max[:], in_=cols[:], axis=AXIS.X, op=ALU.max)
+        max_row = bank(3)
+        nc.tensor.transpose(max_row[:, :P], col_max[:].to_broadcast([P, P]), ident[:])
+        spread = []
+        for h in range(HALVES):
+            spread.append(bank(4 + h))
+            for c in range(4):
+                nc.tensor.transpose(
+                    spread[h][:, P * c : P * (c + 1)], cols[:, 4 * h + c : 4 * h + c + 1].to_broadcast([P, P]), ident[:]
+                )
+        nc.vector.tensor_copy(picked_scale[:, half(1)], scale_table[:].indirect(half_list(1)))
+        for r in range(4):
+            nc.sync.dma_start(out=x_scale[r:P:32, :].bitcast(I32), in_=picked_scale[8 * r : P : 32, :].bitcast(I32))
+        w2_raw.append(load_w2_half(1, "scales_then_w2"))
+
+        def quantize_weight(grouped, label, cuts):
             codes = keep.tile([P, PACK * P], U32, name=label + "_codes", align_bytes=64)
-            scales = keep.tile([P, PACK * P], U8, name=label + "_scales", tag=tag, align_bytes=64)
-            nc.vector.quantize_mx(
-                out=codes[:].bitcast(FP8X4), scales=scales[:], in_=grouped[:].rearrange("p t m j -> p (t m j)")
-            )
+            scales = keep.tile([P, PACK * P], U8, name=label + "_scales", align_bytes=64)
+            for t0, t1 in zip(cuts, cuts[1:]):
+                nc.vector.quantize_mx(
+                    out=codes[:, P * t0 : P * t1].bitcast(FP8X4),
+                    scales=scales[:, P * t0 : P * t1],
+                    in_=grouped[:, t0:t1, :, :].rearrange("p t m j -> p (t m j)"),
+                )
             return codes, scales
 
-        w1_codes, w1_scales = quantize_weight(group_weight(w1_raw, "w1", "w1_then_codes"), "w1", "max_then_scales")
+        w1_codes, w1_scales = quantize_weight(w1_grouped, "w1", (0, 4))
 
-        weights = keep.tile([P, S], F32, name="weights", tag="w1_then_weights")
-        total = keep.tile([P, 1], F32, name="total")
-        nc.scalar.activation(out=weights[:], in_=picked[:], func=ACT.Exp, bias=neg_max[:], scale=1.0, accum_out=total[:])
-
-        x_codes = keep.tile([P, S], U32, name="x_codes", tag="w1_then_codes", align_bytes=64)
+        neg_max = keep.tile([P, 1], F32, name="neg_max")
+        nc.vector.tensor_reduce(out=neg_max[:], in_=max_row[:, :P], axis=AXIS.X, op=ALU.max, negate=True)
+        weights = keep.tile([P, S], F32, name="weights")
+        totals = keep.tile([P, HALVES], F32, name="totals")
         for h in range(HALVES):
-            nc.vector.tensor_copy(
-                x_codes[:, BANK * h : BANK * (h + 1)],
-                word_table[:].bitcast(U32).indirect(offsets[:, h * (BANK // 16) : (h + 1) * (BANK // 16)]),
+            nc.scalar.activation(
+                out=weights[:, half(h)], in_=spread[h][:], func=ACT.Exp, bias=neg_max[:], scale=1.0, accum_out=totals[:, h : h + 1]
             )
 
+        x_codes = keep.tile([P, S], U32, name="x_codes", tag="max_then_codes", align_bytes=64)
+        for h in range(HALVES):
+            nc.vector.tensor_copy(x_codes[:, half(h)], word_table[:].bitcast(U32).indirect(half_list(h)))
+
+        def group_weight(raw, label, copies):
+            grouped = keep.tile([P, PACK, P, PACK], BF16, name=label + "_grouped", align_bytes=64)
+            for u in range(2):
+                copies[u](
+                    out=grouped[:, :, u * (P // 2) : (u + 1) * (P // 2), :].rearrange("p t m j -> p m j t"),
+                    in_=raw[u][:].rearrange("p j (m t) -> p m j t", t=PACK),
+                )
+            return grouped
+
+
+        total = keep.tile([P, 1], F32, name="total")
+        nc.vector.tensor_tensor(out=total[:], in0=totals[:, 0:1], in1=totals[:, 1:2], op=ALU.add)
         inv_total = keep.tile([P, 1], F32, name="inv_total")
         nc.vector.reciprocal(inv_total[:], total[:])
 
@@ -145,15 +164,15 @@ def tile_picked_ygcb_relu_po_kernel(tc, x_words, x_scales, w1, w2, score, offs, 
                     out=y[t, h][:],
                     lhsT=w1_codes[:, P * t : P * (t + 1)].bitcast(FP8X4),
                     lhsT_scale=w1_scales[:, P * t : P * (t + 1)],
-                    rhs=x_codes[:, BANK * h : BANK * (h + 1)].bitcast(FP8X4),
-                    rhs_scale=x_scale[:, BANK * h : BANK * (h + 1)],
+                    rhs=x_codes[:, half(h)].bitcast(FP8X4),
+                    rhs_scale=x_scale[:, half(h)],
                     start=True,
                     stop=True,
                 )
 
-        w2_grouped = group_weight(w2_raw, "w2", "scales_then_picked")
+        w2_grouped = group_weight(w2_raw, "w2", (nc.scalar.copy, nc.scalar.copy))
 
-        z_planes = keep.tile([P, PACK, S], BF16, name="z_planes", tag="w2_then_z")
+        z_planes = keep.tile([P, PACK, S], BF16, name="z_planes", tag="scales_then_w2", align_bytes=64)
         for t in range(PACK):
             part = keep.tile([P, HALVES], F32, name="part%d" % t, align_bytes=64)
             for h in range(HALVES):
@@ -161,14 +180,16 @@ def tile_picked_ygcb_relu_po_kernel(tc, x_words, x_scales, w1, w2, score, offs, 
                 nc.vector.scalar_tensor_tensor(
                     out=weighted[:],
                     in0=y[t, h][:],
-                    scalar=inv_total[:],
-                    in1=weights[:, BANK * h : BANK * (h + 1)],
+                    scalar=1.0,
+                    in1=weights[:, half(h)],
                     op0=ALU.mult,
                     op1=ALU.mult,
                     accum_out=part[:, h : h + 1],
                 )
             context = keep.tile([P, 1], F32, name="context%d" % t)
-            nc.vector.tensor_tensor(out=context[:], in0=part[:, 0:1], in1=part[:, 1:2], op=ALU.add)
+            nc.gpsimd.tensor_scalar(
+                out=context[:], in0=part[:, 0:1], scalar1=part[:, 1:2], scalar2=inv_total[:], op0=ALU.add, op1=ALU.mult
+            )
             cuts = (0, WIDTHS[0], BANK, S) if t == PACK - 1 else (0, BANK, S)
             for c0, c1 in zip(cuts, cuts[1:]):
                 h = c0 // BANK
@@ -180,24 +201,36 @@ def tile_picked_ygcb_relu_po_kernel(tc, x_words, x_scales, w1, w2, score, offs, 
                     scale=1.0,
                 )
 
-        w2_codes, w2_scales = quantize_weight(w2_grouped, "w2", "part1")
-
         out_rows = out_0.rearrange("(p t) j -> p t j", t=PACK)
         out_words = out_1[0].rearrange("p c r -> p (c r)").bitcast(I32)
         out_codes = keep.tile([P, S], I32, name="out_codes", align_bytes=64)
         out_scales = keep.tile([P, S], U8, name="out_scales", align_bytes=64)
+        w2_codes = keep.tile([P, PACK * P], U32, name="w2_codes", align_bytes=64)
+        w2_scales = keep.tile([P, PACK * P], U8, name="w2_scales", align_bytes=64)
+        z_grouped, results, out_grouped = {}, {}, {}
+
+        def chunk(c):
+            return slice(STARTS[c], STARTS[c] + WIDTHS[c])
+
+        def quantize_w2(u):
+            nc.vector.quantize_mx(
+                out=w2_codes[:, 2 * P * u : 2 * P * (u + 1)].bitcast(FP8X4),
+                scales=w2_scales[:, 2 * P * u : 2 * P * (u + 1)],
+                in_=w2_grouped[:, 2 * u : 2 * u + 2, :, :].rearrange("p t m j -> p (t m j)"),
+            )
+
+        def group_z(c):
+            z_grouped[c] = keep.tile([P, WIDTHS[c], PACK], BF16, name="z_grouped%d" % c, align_bytes=64)
+            interleave(nc.scalar.copy if c == SCALAR_Z else nc.vector.tensor_copy, z_grouped[c][:], z_planes[:, :, chunk(c)])
 
         def second_product(c):
             width = WIDTHS[c]
-            cols = slice(STARTS[c], STARTS[c] + width)
-            z_grouped = keep.tile([P, width, PACK], BF16, name="z_grouped%d" % c, align_bytes=64)
-            interleave(nc.scalar.copy if c == CHUNKS - 1 else nc.vector.tensor_copy, z_grouped[:], z_planes[:, :, cols])
             z_codes = keep.tile([P, width], U32, name="z_codes%d" % c, align_bytes=64)
             z_scales = keep.tile([P, width], U8, name="z_scales%d" % c, align_bytes=64)
             nc.vector.quantize_mx(
-                out=z_codes[:].bitcast(FP8X4), scales=z_scales[:], in_=z_grouped[:].rearrange("p c t -> p (c t)")
+                out=z_codes[:].bitcast(FP8X4), scales=z_scales[:], in_=z_grouped[c][:].rearrange("p c t -> p (c t)")
             )
-            result = keep.tile([P, PACK, width], F32, name="result%d" % c)
+            results[c] = keep.tile([P, PACK, width], F32, name="result%d" % c)
             per_bank = BANK // width
             for t0 in range(0, PACK, per_bank):
                 acc = bank((PACK * STARTS[c] + t0 * width) // BANK)
@@ -212,24 +245,37 @@ def tile_picked_ygcb_relu_po_kernel(tc, x_words, x_scales, w1, w2, score, offs, 
                         start=True,
                         stop=True,
                     )
-                nc.scalar.copy(out=result[:, t0 : t0 + per_bank, :].rearrange("p t c -> p (t c)"), in_=acc[:])
-            nc.sync.dma_start(out=out_rows[:, :, cols], in_=result[:])
-            return result
+                nc.scalar.copy(out=results[c][:, t0 : t0 + per_bank, :].rearrange("p t c -> p (t c)"), in_=acc[:])
+            nc.sync.dma_start(out=out_rows[:, :, chunk(c)], in_=results[c][:])
 
-        def hand_on(c, result):
-            width = WIDTHS[c]
-            cols = slice(STARTS[c], STARTS[c] + width)
-            grouped = keep.tile([P, width, PACK], BF16, name="out_grouped%d" % c, align_bytes=64)
-            interleave(nc.vector.tensor_copy, grouped[:], result[:])
+        def group_out(c):
+            out_grouped[c] = keep.tile([P, WIDTHS[c], PACK], BF16, name="out_grouped%d" % c, align_bytes=64)
+            interleave(nc.scalar.copy if c == CHUNKS - 1 else nc.vector.tensor_copy, out_grouped[c][:], results[c][:])
+
+        def hand_on(c):
             nc.vector.quantize_mx(
-                out=out_codes[:, cols].bitcast(FP8X4),
-                scales=out_scales[:, cols],
-                in_=grouped[:].rearrange("p c t -> p (c t)"),
+                out=out_codes[:, chunk(c)].bitcast(FP8X4),
+                scales=out_scales[:, chunk(c)],
+                in_=out_grouped[c][:].rearrange("p c t -> p (c t)"),
             )
 
-        results = [second_product(c) for c in range(CHUNKS)]
-        for c in range(CHUNKS):
-            hand_on(c, results[c])
+        group_z(SCALAR_Z)
+        quantize_w2(0)
+        group_z(0)
+        quantize_w2(1)
+        second_product(0)
+        group_z(1)
+        group_z(2)
+        second_product(1)
+        group_z(4)
+        second_product(2)
+        second_product(3)
+        group_out(0)
+        second_product(4)
+        for c in range(CHUNKS - 1):
+            group_out(c + 1)
+            hand_on(c)
+        hand_on(CHUNKS - 1)
         early = STARTS[3]
         nc.sync.dma_start(out=out_words[:, :early], in_=out_codes[:, :early])
         nc.sync.dma_start(out=out_words[:, early:], in_=out_codes[:, early:])

@@ -27,7 +27,6 @@ CHUNKS = len(WIDTHS)
 QUADS = 4
 RUN = 4
 ROW = P - 1
-SCALAR_Z = 3
 
 
 def interleave(engine_copy, out, planes):
@@ -63,6 +62,7 @@ def tile_picked_ygcb_relu_po_kernel(tc, x_words, x_scales, w1, w2, score, offs, 
         word_table = keep.tile([P, T], I32, name="word_table", align_bytes=64)
         nc.sync.dma_start(out=word_table[:], in_=x_words[0].rearrange("p c r -> p (c r)").bitcast(I32))
 
+
         def load_w2_half(u, tag):
             raw = keep.tile([P, PACK, N // 2], F32, name="w2_raw%d" % u, tag=tag, align_bytes=64)
             nc.sync.dma_start(out=raw[:], in_=w2.rearrange("(p j) c -> p j c", j=PACK)[:, :, u * (N // 2) : (u + 1) * (N // 2)])
@@ -90,17 +90,19 @@ def tile_picked_ygcb_relu_po_kernel(tc, x_words, x_scales, w1, w2, score, offs, 
         picked = keep.tile([P, S], F32, name="picked")
         for h in range(HALVES):
             nc.vector.tensor_copy(picked[:, half(h)], score_table[:].indirect(half_list(h)))
-        cols = keep.tile([P, S // P], F32, name="cols")
+        cols = keep.tile([P, S // P], F32, name="cols", tag="cols_then_codes", align_bytes=64)
+        max_cols = keep.tile([P, S // P], F32, name="max_cols", tag="w1_scales", align_bytes=64)
         for h in range(HALVES):
             turned = bank(6 + h)
             for c in range(4):
                 nc.tensor.transpose(turned[:, P * c : P * (c + 1)], picked[:, BANK * h + P * c : BANK * h + P * (c + 1)], ident[:])
-            nc.scalar.copy(out=cols[:, 4 * h : 4 * h + 4], in_=turned[:].rearrange("p (c n) -> p c n", c=4)[:, :, ROW])
+            for copy in (max_cols, cols):
+                nc.scalar.copy(out=copy[:, 4 * h : 4 * h + 4], in_=turned[:].rearrange("p (c n) -> p c n", c=4)[:, :, ROW])
 
         picked_scale = keep.tile([P, S], U8, name="picked_scale", align_bytes=64)
         nc.vector.tensor_copy(picked_scale[:, half(0)], scale_table[:].indirect(half_list(0)))
         col_max = keep.tile([P, 1], F32, name="col_max", tag="max_then_codes", align_bytes=64)
-        nc.vector.tensor_reduce(out=col_max[:], in_=cols[:], axis=AXIS.X, op=ALU.max)
+        nc.vector.tensor_reduce(out=col_max[:], in_=max_cols[:], axis=AXIS.X, op=ALU.max)
         max_row = bank(3)
         nc.tensor.transpose(max_row[:, :P], col_max[:].to_broadcast([P, P]), ident[:])
         spread = []
@@ -117,7 +119,7 @@ def tile_picked_ygcb_relu_po_kernel(tc, x_words, x_scales, w1, w2, score, offs, 
 
         def quantize_weight(grouped, label, cuts):
             codes = keep.tile([P, PACK * P], U32, name=label + "_codes", align_bytes=64)
-            scales = keep.tile([P, PACK * P], U8, name=label + "_scales", align_bytes=64)
+            scales = keep.tile([P, PACK * P], U8, name=label + "_scales", tag=label + "_scales", align_bytes=64)
             for t0, t1 in zip(cuts, cuts[1:]):
                 nc.vector.quantize_mx(
                     out=codes[:, P * t0 : P * t1].bitcast(FP8X4),
@@ -128,7 +130,7 @@ def tile_picked_ygcb_relu_po_kernel(tc, x_words, x_scales, w1, w2, score, offs, 
 
         w1_codes, w1_scales = quantize_weight(w1_grouped, "w1", (0, 4))
 
-        neg_max = keep.tile([P, 1], F32, name="neg_max")
+        neg_max = keep.tile([P, 1], F32, name="neg_max", tag="w2_grouped", align_bytes=64)
         nc.vector.tensor_reduce(out=neg_max[:], in_=max_row[:, :P], axis=AXIS.X, op=ALU.max, negate=True)
         weights = keep.tile([P, S], F32, name="weights")
         totals = keep.tile([P, HALVES], F32, name="totals")
@@ -137,12 +139,13 @@ def tile_picked_ygcb_relu_po_kernel(tc, x_words, x_scales, w1, w2, score, offs, 
                 out=weights[:, half(h)], in_=spread[h][:], func=ACT.Exp, bias=neg_max[:], scale=1.0, accum_out=totals[:, h : h + 1]
             )
 
-        x_codes = keep.tile([P, S], U32, name="x_codes", tag="max_then_codes", align_bytes=64)
-        for h in range(HALVES):
-            nc.vector.tensor_copy(x_codes[:, half(h)], word_table[:].bitcast(U32).indirect(half_list(h)))
+        x_codes = []
+        for h, tag in enumerate(("max_then_codes", "cols_then_codes")):
+            x_codes.append(keep.tile([P, BANK], U32, name="x_codes%d" % h, tag=tag, align_bytes=64))
+            nc.vector.tensor_copy(x_codes[h][:], word_table[:].bitcast(U32).indirect(half_list(h)))
 
         def group_weight(raw, label, copies):
-            grouped = keep.tile([P, PACK, P, PACK], BF16, name=label + "_grouped", align_bytes=64)
+            grouped = keep.tile([P, PACK, P, PACK], BF16, name=label + "_grouped", tag=label + "_grouped", align_bytes=64)
             for u in range(2):
                 copies[u](
                     out=grouped[:, :, u * (P // 2) : (u + 1) * (P // 2), :].rearrange("p t m j -> p m j t"),
@@ -152,19 +155,18 @@ def tile_picked_ygcb_relu_po_kernel(tc, x_words, x_scales, w1, w2, score, offs, 
 
 
         total = keep.tile([P, 1], F32, name="total")
-        nc.vector.tensor_tensor(out=total[:], in0=totals[:, 0:1], in1=totals[:, 1:2], op=ALU.add)
-        inv_total = keep.tile([P, 1], F32, name="inv_total")
-        nc.vector.reciprocal(inv_total[:], total[:])
+        nc.gpsimd.tensor_tensor(out=total[:], in0=totals[:, 0:1], in1=totals[:, 1:2], op=ALU.add)
 
         y = {}
-        for t in range(PACK):
-            for h in range(HALVES):
+        order = [(t, h) for t in range(PACK) for h in range(HALVES)]
+        for t, h in order:
+            if True:
                 y[t, h] = bank(HALVES * t + h)
                 nc.tensor.matmul_mx(
                     out=y[t, h][:],
                     lhsT=w1_codes[:, P * t : P * (t + 1)].bitcast(FP8X4),
                     lhsT_scale=w1_scales[:, P * t : P * (t + 1)],
-                    rhs=x_codes[:, half(h)].bitcast(FP8X4),
+                    rhs=x_codes[h][:].bitcast(FP8X4),
                     rhs_scale=x_scale[:, half(h)],
                     start=True,
                     stop=True,
@@ -173,22 +175,24 @@ def tile_picked_ygcb_relu_po_kernel(tc, x_words, x_scales, w1, w2, score, offs, 
         w2_grouped = group_weight(w2_raw, "w2", (nc.scalar.copy, nc.scalar.copy))
 
         z_planes = keep.tile([P, PACK, S], BF16, name="z_planes", tag="scales_then_w2", align_bytes=64)
-        for t in range(PACK):
-            part = keep.tile([P, HALVES], F32, name="part%d" % t, align_bytes=64)
-            for h in range(HALVES):
-                weighted = keep.tile([P, BANK], BF16, name="weighted%d_%d" % (t, h))
-                nc.vector.scalar_tensor_tensor(
-                    out=weighted[:],
-                    in0=y[t, h][:],
-                    scalar=1.0,
-                    in1=weights[:, half(h)],
-                    op0=ALU.mult,
-                    op1=ALU.mult,
-                    accum_out=part[:, h : h + 1],
-                )
+        parts = [keep.tile([P, HALVES], F32, name="part%d" % t) for t in range(PACK)]
+
+        def weighted_sum(t, h):
+            weighted = keep.tile([P, BANK], BF16, name="weighted%d_%d" % (t, h), tag="weighted%d_%d" % (t, h))
+            nc.vector.scalar_tensor_tensor(
+                out=weighted[:],
+                in0=y[t, h][:],
+                scalar=1.0,
+                in1=weights[:, half(h)],
+                op0=ALU.mult,
+                op1=ALU.mult,
+                accum_out=parts[t][:, h : h + 1],
+            )
+
+        def add_context(t):
             context = keep.tile([P, 1], F32, name="context%d" % t)
             nc.gpsimd.tensor_scalar(
-                out=context[:], in0=part[:, 0:1], scalar1=part[:, 1:2], scalar2=inv_total[:], op0=ALU.add, op1=ALU.mult
+                out=context[:], in0=parts[t][:, 0:1], scalar1=parts[t][:, 1:2], scalar2=inv_total[:], op0=ALU.add, op1=ALU.mult
             )
             cuts = (0, WIDTHS[0], BANK, S) if t == PACK - 1 else (0, BANK, S)
             for c0, c1 in zip(cuts, cuts[1:]):
@@ -200,6 +204,14 @@ def tile_picked_ygcb_relu_po_kernel(tc, x_words, x_scales, w1, w2, score, offs, 
                     bias=context[:],
                     scale=1.0,
                 )
+
+        weighted_sum(*order[0])
+        inv_total = keep.tile([P, 1], F32, name="inv_total", tag="weighted0_0")
+        nc.vector.reciprocal(inv_total[:], total[:])
+        for t, h in order[1:]:
+            weighted_sum(t, h)
+            if h == HALVES - 1:
+                add_context(t)
 
         out_rows = out_0.rearrange("(p t) j -> p t j", t=PACK)
         out_words = out_1[0].rearrange("p c r -> p (c r)").bitcast(I32)
@@ -221,7 +233,7 @@ def tile_picked_ygcb_relu_po_kernel(tc, x_words, x_scales, w1, w2, score, offs, 
 
         def group_z(c):
             z_grouped[c] = keep.tile([P, WIDTHS[c], PACK], BF16, name="z_grouped%d" % c, align_bytes=64)
-            interleave(nc.scalar.copy if c == SCALAR_Z else nc.vector.tensor_copy, z_grouped[c][:], z_planes[:, :, chunk(c)])
+            interleave(nc.scalar.copy if c == CHUNKS - 1 else nc.vector.tensor_copy, z_grouped[c][:], z_planes[:, :, chunk(c)])
 
         def second_product(c):
             width = WIDTHS[c]
@@ -259,19 +271,18 @@ def tile_picked_ygcb_relu_po_kernel(tc, x_words, x_scales, w1, w2, score, offs, 
                 in_=out_grouped[c][:].rearrange("p c t -> p (c t)"),
             )
 
-        group_z(SCALAR_Z)
+        group_z(CHUNKS - 1)
         quantize_w2(0)
         group_z(0)
         quantize_w2(1)
         second_product(0)
         group_z(1)
-        group_z(2)
-        second_product(1)
-        group_z(4)
-        second_product(2)
-        second_product(3)
+        for c in range(1, CHUNKS - 2):
+            group_z(c + 1)
+            second_product(c)
+        second_product(CHUNKS - 2)
         group_out(0)
-        second_product(4)
+        second_product(CHUNKS - 1)
         for c in range(CHUNKS - 1):
             group_out(c + 1)
             hand_on(c)

@@ -24,9 +24,13 @@ HALVES = S // BANK
 WIDTHS = (128, 256, 256, 256, 128)
 STARTS = tuple(sum(WIDTHS[:c]) for c in range(len(WIDTHS)))
 CHUNKS = len(WIDTHS)
+OUT_WIDTHS = (256, 256, 256, 128, 128)
+OUT_STARTS = tuple(sum(OUT_WIDTHS[:c]) for c in range(len(OUT_WIDTHS)))
 QUADS = 4
 RUN = 4
 ROW = P - 1
+VECTOR_END = 2559
+SCALAR_END = 3584
 
 
 def interleave(engine_copy, out, planes):
@@ -49,11 +53,15 @@ def tile_picked_ygcb_relu_po_kernel(tc, x_words, x_scales, w1, w2, score, offs, 
         nc.sync.dma_start(offsets[:], offs)
 
         scale_table = keep.tile([P, T], U8, name="scale_table", tag="scales_then_w2", align_bytes=64)
-        nc.vector.memset(scale_table[:].bitcast(I32), 0)
+        zero = keep.tile([P, 1], F32, name="zero")
+        nc.gpsimd.memset(zero[:], 0.0)
+        nc.gpsimd.memset(scale_table[:].bitcast(I32), 0)
         score_table = keep.tile([P, T], F32, name="score_table")
-        nc.vector.memset(score_table[:ROW, :].bitcast(I32), 0)
+        nc.vector.memset(score_table[:ROW, :VECTOR_END].bitcast(I32), 0)
+        nc.scalar.copy(out=score_table[:ROW, VECTOR_END:SCALAR_END], in_=zero[:ROW, :].to_broadcast([ROW, SCALAR_END - VECTOR_END]))
+        nc.gpsimd.memset(score_table[:ROW, SCALAR_END:].bitcast(I32), 0)
         x_scale = keep.tile([P, S], U8, name="x_scale", align_bytes=64)
-        nc.vector.memset(x_scale[:].bitcast(I32), 0)
+        nc.gpsimd.memset(x_scale[:].bitcast(I32), 0)
 
         nc.sync.dma_start(out=score_table[ROW:, :], in_=score[0:1, :])
         w1_raw = keep.tile([P, PACK, H], F32, name="w1_raw")
@@ -74,7 +82,7 @@ def tile_picked_ygcb_relu_po_kernel(tc, x_words, x_scales, w1, w2, score, offs, 
         make_identity(nc, ident[:])
 
         warm = keep.tile([P, 1], F32, name="warm")
-        nc.scalar.activation(out=warm[:], in_=ident[:, 0:1], func=ACT.Exp)
+        nc.scalar.activation(out=warm[:], in_=zero[:], func=ACT.Exp)
 
         def half(h):
             return slice(BANK * h, BANK * (h + 1))
@@ -216,10 +224,11 @@ def tile_picked_ygcb_relu_po_kernel(tc, x_words, x_scales, w1, w2, score, offs, 
         out_rows = out_0.rearrange("(p t) j -> p t j", t=PACK)
         out_words = out_1[0].rearrange("p c r -> p (c r)").bitcast(I32)
         out_codes = keep.tile([P, S], I32, name="out_codes", align_bytes=64)
-        out_scales = keep.tile([P, S], U8, name="out_scales", align_bytes=64)
+        out_scales = keep.tile([P, S // QUADS], U8, name="out_scales", align_bytes=64)
+        result = keep.tile([P, PACK, S], F32, name="result")
         w2_codes = keep.tile([P, PACK * P], U32, name="w2_codes", align_bytes=64)
         w2_scales = keep.tile([P, PACK * P], U8, name="w2_scales", align_bytes=64)
-        z_grouped, results, out_grouped = {}, {}, {}
+        z_grouped, out_grouped = {}, {}
 
         def chunk(c):
             return slice(STARTS[c], STARTS[c] + WIDTHS[c])
@@ -242,7 +251,6 @@ def tile_picked_ygcb_relu_po_kernel(tc, x_words, x_scales, w1, w2, score, offs, 
             nc.vector.quantize_mx(
                 out=z_codes[:].bitcast(FP8X4), scales=z_scales[:], in_=z_grouped[c][:].rearrange("p c t -> p (c t)")
             )
-            results[c] = keep.tile([P, PACK, width], F32, name="result%d" % c)
             per_bank = BANK // width
             for t0 in range(0, PACK, per_bank):
                 acc = bank((PACK * STARTS[c] + t0 * width) // BANK)
@@ -257,17 +265,21 @@ def tile_picked_ygcb_relu_po_kernel(tc, x_words, x_scales, w1, w2, score, offs, 
                         start=True,
                         stop=True,
                     )
-                nc.scalar.copy(out=results[c][:, t0 : t0 + per_bank, :].rearrange("p t c -> p (t c)"), in_=acc[:])
-            nc.sync.dma_start(out=out_rows[:, :, chunk(c)], in_=results[c][:])
+                nc.scalar.copy(out=result[:, t0 : t0 + per_bank, chunk(c)], in_=acc[:].rearrange("p (t c) -> p t c", t=per_bank))
+            nc.sync.dma_start(out=out_rows[:, :, chunk(c)], in_=result[:, :, chunk(c)])
+
+        def out_chunk(c):
+            return slice(OUT_STARTS[c], OUT_STARTS[c] + OUT_WIDTHS[c])
 
         def group_out(c):
-            out_grouped[c] = keep.tile([P, WIDTHS[c], PACK], BF16, name="out_grouped%d" % c, align_bytes=64)
-            interleave(nc.scalar.copy if c == CHUNKS - 1 else nc.vector.tensor_copy, out_grouped[c][:], results[c][:])
+            out_grouped[c] = keep.tile([P, OUT_WIDTHS[c], PACK], BF16, name="out_grouped%d" % c, align_bytes=64)
+            interleave(nc.scalar.copy if c == CHUNKS - 1 else nc.vector.tensor_copy, out_grouped[c][:], result[:, :, out_chunk(c)])
 
         def hand_on(c):
+            plane, first = divmod(OUT_STARTS[c], S // QUADS)
             nc.vector.quantize_mx(
-                out=out_codes[:, chunk(c)].bitcast(FP8X4),
-                scales=out_scales[:, chunk(c)],
+                out=out_codes[:, out_chunk(c)].bitcast(FP8X4),
+                scales=out_scales[4 * plane :, first : first + OUT_WIDTHS[c]],
                 in_=out_grouped[c][:].rearrange("p c t -> p (c t)"),
             )
 
@@ -281,18 +293,18 @@ def tile_picked_ygcb_relu_po_kernel(tc, x_words, x_scales, w1, w2, score, offs, 
             group_z(c + 1)
             second_product(c)
         second_product(CHUNKS - 2)
-        group_out(0)
         second_product(CHUNKS - 1)
+        group_out(0)
         for c in range(CHUNKS - 1):
             group_out(c + 1)
             hand_on(c)
         hand_on(CHUNKS - 1)
-        early = STARTS[3]
+        early = OUT_STARTS[3]
         nc.sync.dma_start(out=out_words[:, :early], in_=out_codes[:, :early])
         nc.sync.dma_start(out=out_words[:, early:], in_=out_codes[:, early:])
         for q in range(QUADS):
             queue = nc.sync if q % 2 == 0 else nc.scalar
             queue.dma_start(
-                out=out_2[0, 4 * q : 4 * q + 4, :].bitcast(I32),
-                in_=out_scales[32 * q : 32 * q + 4, :].bitcast(I32),
+                out=out_2[0, 4 * q : 4 * q + 4, :].bitcast(I32).rearrange("r (j n) -> j r n", j=QUADS),
+                in_=out_scales[32 * q : 32 * q + 16, :].bitcast(I32),
             )

@@ -21,7 +21,7 @@ P = 128
 PACK = 4
 BANK = 512
 HALVES = S // BANK
-WIDTHS = (128, 256, 256, 256, 128)
+WIDTHS = (128, 128, 256, 256, 128, 128)
 STARTS = tuple(sum(WIDTHS[:c]) for c in range(len(WIDTHS)))
 CHUNKS = len(WIDTHS)
 OUT_WIDTHS = (256, 256, 256, 128, 128)
@@ -29,8 +29,8 @@ OUT_STARTS = tuple(sum(OUT_WIDTHS[:c]) for c in range(len(OUT_WIDTHS)))
 QUADS = 4
 RUN = 4
 ROW = P - 1
-VECTOR_END = 2559
-SCALAR_END = 3584
+SLOW_END = 1023
+VECTOR_END = 3583
 
 
 def interleave(engine_copy, out, planes):
@@ -57,9 +57,11 @@ def tile_picked_ygcb_relu_po_kernel(tc, x_words, x_scales, w1, w2, score, offs, 
         nc.gpsimd.memset(zero[:], 0.0)
         nc.gpsimd.memset(scale_table[:].bitcast(I32), 0)
         score_table = keep.tile([P, T], F32, name="score_table")
-        nc.vector.memset(score_table[:ROW, :VECTOR_END].bitcast(I32), 0)
-        nc.scalar.copy(out=score_table[:ROW, VECTOR_END:SCALAR_END], in_=zero[:ROW, :].to_broadcast([ROW, SCALAR_END - VECTOR_END]))
-        nc.gpsimd.memset(score_table[:ROW, SCALAR_END:].bitcast(I32), 0)
+        nc.vector.memset(score_table[:ROW, :SLOW_END].bitcast(I32), 0)
+        nc.vector.memset(score_table[:ROW, SLOW_END:VECTOR_END].bitcast(I32), 0)
+        nc.scalar.copy(out=score_table[:ROW, VECTOR_END:], in_=zero[:ROW, :].to_broadcast([ROW, T - VECTOR_END]))
+        ident = keep.tile([P, P], F32, name="ident")
+        make_identity(nc, ident[:])
         x_scale = keep.tile([P, S], U8, name="x_scale", align_bytes=64)
         nc.gpsimd.memset(x_scale[:].bitcast(I32), 0)
 
@@ -78,9 +80,6 @@ def tile_picked_ygcb_relu_po_kernel(tc, x_words, x_scales, w1, w2, score, offs, 
 
         w2_raw = [load_w2_half(0, "w2_first_half")]
 
-        ident = keep.tile([P, P], F32, name="ident")
-        make_identity(nc, ident[:])
-
         warm = keep.tile([P, 1], F32, name="warm")
         nc.scalar.activation(out=warm[:], in_=zero[:], func=ACT.Exp)
 
@@ -98,7 +97,7 @@ def tile_picked_ygcb_relu_po_kernel(tc, x_words, x_scales, w1, w2, score, offs, 
         picked = keep.tile([P, S], F32, name="picked")
         for h in range(HALVES):
             nc.vector.tensor_copy(picked[:, half(h)], score_table[:].indirect(half_list(h)))
-        cols = keep.tile([P, S // P], F32, name="cols", tag="cols_then_codes", align_bytes=64)
+        cols = keep.tile([P, S // P], F32, name="cols", tag="cols", align_bytes=64)
         max_cols = keep.tile([P, S // P], F32, name="max_cols", tag="w1_scales", align_bytes=64)
         for h in range(HALVES):
             turned = bank(6 + h)
@@ -111,15 +110,8 @@ def tile_picked_ygcb_relu_po_kernel(tc, x_words, x_scales, w1, w2, score, offs, 
         nc.vector.tensor_copy(picked_scale[:, half(0)], scale_table[:].indirect(half_list(0)))
         col_max = keep.tile([P, 1], F32, name="col_max", tag="max_then_codes", align_bytes=64)
         nc.vector.tensor_reduce(out=col_max[:], in_=max_cols[:], axis=AXIS.X, op=ALU.max)
-        max_row = bank(3)
+        max_row = bank(4)
         nc.tensor.transpose(max_row[:, :P], col_max[:].to_broadcast([P, P]), ident[:])
-        spread = []
-        for h in range(HALVES):
-            spread.append(bank(4 + h))
-            for c in range(4):
-                nc.tensor.transpose(
-                    spread[h][:, P * c : P * (c + 1)], cols[:, 4 * h + c : 4 * h + c + 1].to_broadcast([P, P]), ident[:]
-                )
         nc.vector.tensor_copy(picked_scale[:, half(1)], scale_table[:].indirect(half_list(1)))
         for r in range(4):
             nc.sync.dma_start(out=x_scale[r:P:32, :].bitcast(I32), in_=picked_scale[8 * r : P : 32, :].bitcast(I32))
@@ -140,6 +132,13 @@ def tile_picked_ygcb_relu_po_kernel(tc, x_words, x_scales, w1, w2, score, offs, 
 
         neg_max = keep.tile([P, 1], F32, name="neg_max", tag="w2_grouped", align_bytes=64)
         nc.vector.tensor_reduce(out=neg_max[:], in_=max_row[:, :P], axis=AXIS.X, op=ALU.max, negate=True)
+        spread = []
+        for h in range(HALVES):
+            spread.append(bank(4 + h))
+            for c in range(4):
+                nc.tensor.transpose(
+                    spread[h][:, P * c : P * (c + 1)], cols[:, 4 * h + c : 4 * h + c + 1].to_broadcast([P, P]), ident[:]
+                )
         weights = keep.tile([P, S], F32, name="weights")
         totals = keep.tile([P, HALVES], F32, name="totals")
         for h in range(HALVES):
@@ -147,10 +146,9 @@ def tile_picked_ygcb_relu_po_kernel(tc, x_words, x_scales, w1, w2, score, offs, 
                 out=weights[:, half(h)], in_=spread[h][:], func=ACT.Exp, bias=neg_max[:], scale=1.0, accum_out=totals[:, h : h + 1]
             )
 
-        x_codes = []
-        for h, tag in enumerate(("max_then_codes", "cols_then_codes")):
-            x_codes.append(keep.tile([P, BANK], U32, name="x_codes%d" % h, tag=tag, align_bytes=64))
-            nc.vector.tensor_copy(x_codes[h][:], word_table[:].bitcast(U32).indirect(half_list(h)))
+        x_codes = keep.tile([P, S], U32, name="x_codes", tag="max_then_codes", align_bytes=64)
+        for h in range(HALVES):
+            nc.vector.tensor_copy(x_codes[:, half(h)], word_table[:].bitcast(U32).indirect(half_list(h)))
 
         def group_weight(raw, label, copies):
             grouped = keep.tile([P, PACK, P, PACK], BF16, name=label + "_grouped", tag=label + "_grouped", align_bytes=64)
@@ -174,7 +172,7 @@ def tile_picked_ygcb_relu_po_kernel(tc, x_words, x_scales, w1, w2, score, offs, 
                     out=y[t, h][:],
                     lhsT=w1_codes[:, P * t : P * (t + 1)].bitcast(FP8X4),
                     lhsT_scale=w1_scales[:, P * t : P * (t + 1)],
-                    rhs=x_codes[h][:].bitcast(FP8X4),
+                    rhs=x_codes[:, half(h)].bitcast(FP8X4),
                     rhs_scale=x_scale[:, half(h)],
                     start=True,
                     stop=True,
@@ -202,7 +200,7 @@ def tile_picked_ygcb_relu_po_kernel(tc, x_words, x_scales, w1, w2, score, offs, 
             nc.gpsimd.tensor_scalar(
                 out=context[:], in0=parts[t][:, 0:1], scalar1=parts[t][:, 1:2], scalar2=inv_total[:], op0=ALU.add, op1=ALU.mult
             )
-            cuts = (0, WIDTHS[0], BANK, S) if t == PACK - 1 else (0, BANK, S)
+            cuts = (0, STARTS[1], STARTS[2], BANK, S) if t == PACK - 1 else (0, BANK, S)
             for c0, c1 in zip(cuts, cuts[1:]):
                 h = c0 // BANK
                 nc.scalar.activation(
@@ -273,7 +271,7 @@ def tile_picked_ygcb_relu_po_kernel(tc, x_words, x_scales, w1, w2, score, offs, 
 
         def group_out(c):
             out_grouped[c] = keep.tile([P, OUT_WIDTHS[c], PACK], BF16, name="out_grouped%d" % c, align_bytes=64)
-            interleave(nc.scalar.copy if c == CHUNKS - 1 else nc.vector.tensor_copy, out_grouped[c][:], result[:, :, out_chunk(c)])
+            interleave(nc.scalar.copy if c == len(OUT_WIDTHS) - 1 else nc.vector.tensor_copy, out_grouped[c][:], result[:, :, out_chunk(c)])
 
         def hand_on(c):
             plane, first = divmod(OUT_STARTS[c], S // QUADS)
@@ -295,10 +293,10 @@ def tile_picked_ygcb_relu_po_kernel(tc, x_words, x_scales, w1, w2, score, offs, 
         second_product(CHUNKS - 2)
         second_product(CHUNKS - 1)
         group_out(0)
-        for c in range(CHUNKS - 1):
+        for c in range(len(OUT_WIDTHS) - 1):
             group_out(c + 1)
             hand_on(c)
-        hand_on(CHUNKS - 1)
+        hand_on(len(OUT_WIDTHS) - 1)
         early = OUT_STARTS[3]
         nc.sync.dma_start(out=out_words[:, :early], in_=out_codes[:, :early])
         nc.sync.dma_start(out=out_words[:, early:], in_=out_codes[:, early:])

@@ -21,7 +21,8 @@ P = 128
 PACK = 4
 BANK = 512
 HALVES = S // BANK
-WIDTHS = (128, 128, 256, 256, 128, 128)
+WIDTHS = (64, 64, 128, 256, 256, 128, 128)
+FIRST_BANKS = (0, 1, 2, 3, 5, 6, 7)
 STARTS = tuple(sum(WIDTHS[:c]) for c in range(len(WIDTHS)))
 CHUNKS = len(WIDTHS)
 OUT_WIDTHS = (256, 256, 256, 128, 128)
@@ -69,7 +70,7 @@ def tile_picked_ygcb_relu_po_kernel(tc, x_words, x_scales, w1, w2, score, offs, 
         w1_raw = keep.tile([P, PACK, H], F32, name="w1_raw")
         nc.sync.dma_start(out=w1_raw[:], in_=w1.rearrange("(p j) c -> p j c", j=PACK))
         nc.sync.dma_start(out=scale_table[0:P:8, :].bitcast(I32), in_=x_scales[0].bitcast(I32))
-        word_table = keep.tile([P, T], I32, name="word_table", align_bytes=64)
+        word_table = keep.tile([P, T], I32, name="word_table", tag="words_then_scales", align_bytes=64)
         nc.sync.dma_start(out=word_table[:], in_=x_words[0].rearrange("p c r -> p (c r)").bitcast(I32))
 
 
@@ -117,18 +118,17 @@ def tile_picked_ygcb_relu_po_kernel(tc, x_words, x_scales, w1, w2, score, offs, 
             nc.sync.dma_start(out=x_scale[r:P:32, :].bitcast(I32), in_=picked_scale[8 * r : P : 32, :].bitcast(I32))
         w2_raw.append(load_w2_half(1, "scales_then_w2"))
 
-        def quantize_weight(grouped, label, cuts):
-            codes = keep.tile([P, PACK * P], U32, name=label + "_codes", align_bytes=64)
-            scales = keep.tile([P, PACK * P], U8, name=label + "_scales", tag=label + "_scales", align_bytes=64)
-            for t0, t1 in zip(cuts, cuts[1:]):
-                nc.vector.quantize_mx(
-                    out=codes[:, P * t0 : P * t1].bitcast(FP8X4),
-                    scales=scales[:, P * t0 : P * t1],
-                    in_=grouped[:, t0:t1, :, :].rearrange("p t m j -> p (t m j)"),
-                )
+        def quantize_w1(u, tag):
+            codes = keep.tile([P, 2 * P], U32, name="w1_codes%d" % u, align_bytes=64)
+            scales = keep.tile([P, 2 * P], U8, name="w1_scales%d" % u, tag=tag, align_bytes=64)
+            nc.vector.quantize_mx(
+                out=codes[:].bitcast(FP8X4),
+                scales=scales[:],
+                in_=w1_grouped[:, 2 * u : 2 * u + 2, :, :].rearrange("p t m j -> p (t m j)"),
+            )
             return codes, scales
 
-        w1_codes, w1_scales = quantize_weight(w1_grouped, "w1", (0, 4))
+        w1_mx = [quantize_w1(0, "w1_scales")]
 
         neg_max = keep.tile([P, 1], F32, name="neg_max", tag="w2_grouped", align_bytes=64)
         nc.vector.tensor_reduce(out=neg_max[:], in_=max_row[:, :P], axis=AXIS.X, op=ALU.max, negate=True)
@@ -149,6 +149,7 @@ def tile_picked_ygcb_relu_po_kernel(tc, x_words, x_scales, w1, w2, score, offs, 
         x_codes = keep.tile([P, S], U32, name="x_codes", tag="max_then_codes", align_bytes=64)
         for h in range(HALVES):
             nc.vector.tensor_copy(x_codes[:, half(h)], word_table[:].bitcast(U32).indirect(half_list(h)))
+        w1_mx.append(quantize_w1(1, "words_then_scales"))
 
         def group_weight(raw, label, copies):
             grouped = keep.tile([P, PACK, P, PACK], BF16, name=label + "_grouped", tag=label + "_grouped", align_bytes=64)
@@ -170,8 +171,8 @@ def tile_picked_ygcb_relu_po_kernel(tc, x_words, x_scales, w1, w2, score, offs, 
                 y[t, h] = bank(HALVES * t + h)
                 nc.tensor.matmul_mx(
                     out=y[t, h][:],
-                    lhsT=w1_codes[:, P * t : P * (t + 1)].bitcast(FP8X4),
-                    lhsT_scale=w1_scales[:, P * t : P * (t + 1)],
+                    lhsT=w1_mx[t // 2][0][:, P * (t % 2) : P * (t % 2 + 1)].bitcast(FP8X4),
+                    lhsT_scale=w1_mx[t // 2][1][:, P * (t % 2) : P * (t % 2 + 1)],
                     rhs=x_codes[:, half(h)].bitcast(FP8X4),
                     rhs_scale=x_scale[:, half(h)],
                     start=True,
@@ -197,10 +198,11 @@ def tile_picked_ygcb_relu_po_kernel(tc, x_words, x_scales, w1, w2, score, offs, 
 
         def add_context(t):
             context = keep.tile([P, 1], F32, name="context%d" % t)
-            nc.gpsimd.tensor_scalar(
+            engine = nc.vector if t == PACK - 1 else nc.gpsimd
+            engine.tensor_scalar(
                 out=context[:], in0=parts[t][:, 0:1], scalar1=parts[t][:, 1:2], scalar2=inv_total[:], op0=ALU.add, op1=ALU.mult
             )
-            cuts = (0, STARTS[1], STARTS[2], BANK, S) if t == PACK - 1 else (0, BANK, S)
+            cuts = STARTS[:5] + (S,) if t == PACK - 1 else (0, BANK, S)
             for c0, c1 in zip(cuts, cuts[1:]):
                 h = c0 // BANK
                 nc.scalar.activation(
@@ -249,9 +251,9 @@ def tile_picked_ygcb_relu_po_kernel(tc, x_words, x_scales, w1, w2, score, offs, 
             nc.vector.quantize_mx(
                 out=z_codes[:].bitcast(FP8X4), scales=z_scales[:], in_=z_grouped[c][:].rearrange("p c t -> p (c t)")
             )
-            per_bank = BANK // width
+            per_bank = min(PACK, BANK // width)
             for t0 in range(0, PACK, per_bank):
-                acc = bank((PACK * STARTS[c] + t0 * width) // BANK)
+                acc = bank((FIRST_BANKS[c] + t0 // per_bank) % 6 if width == 256 else FIRST_BANKS[c])
                 for v in range(per_bank):
                     t = t0 + v
                     nc.tensor.matmul_mx(
@@ -263,7 +265,7 @@ def tile_picked_ygcb_relu_po_kernel(tc, x_words, x_scales, w1, w2, score, offs, 
                         start=True,
                         stop=True,
                     )
-                nc.scalar.copy(out=result[:, t0 : t0 + per_bank, chunk(c)], in_=acc[:].rearrange("p (t c) -> p t c", t=per_bank))
+                nc.scalar.copy(out=result[:, t0 : t0 + per_bank, chunk(c)], in_=acc[:, : per_bank * width].rearrange("p (t c) -> p t c", t=per_bank))
             nc.sync.dma_start(out=out_rows[:, :, chunk(c)], in_=result[:, :, chunk(c)])
 
         def out_chunk(c):

@@ -45,6 +45,7 @@ def tile_picked_ygcb_relu_po_kernel(tc, x_words, x_scales, w1, w2, score, offs, 
     nc = tc.nc
     with ExitStack() as ctx:
         keep = ctx.enter_context(tc.tile_pool(name="keep", bufs=1))
+        shared = ctx.enter_context(tc.tile_pool(name="shared", bufs=1))
         psum = ctx.enter_context(tc.psum_pool(name="psum", bufs=1))
 
         def bank(b):
@@ -98,29 +99,30 @@ def tile_picked_ygcb_relu_po_kernel(tc, x_words, x_scales, w1, w2, score, offs, 
         picked = keep.tile([P, S], F32, name="picked")
         for h in range(HALVES):
             nc.vector.tensor_copy(picked[:, half(h)], score_table[:].indirect(half_list(h)))
-        cols = keep.tile([P, S // P], F32, name="cols", tag="cols", align_bytes=64)
-        max_cols = keep.tile([P, S // P], F32, name="max_cols", tag="w1_scales", align_bytes=64)
+        max_cols = shared.tile([P, P], F32, name="max_cols", offset=0, align_bytes=64)
+        turned = []
         for h in range(HALVES):
-            turned = bank(6 + h)
+            turned.append(bank(6 + h))
             for c in range(4):
-                nc.tensor.transpose(turned[:, P * c : P * (c + 1)], picked[:, BANK * h + P * c : BANK * h + P * (c + 1)], ident[:])
-            for copy in (max_cols, cols):
-                nc.scalar.copy(out=copy[:, 4 * h : 4 * h + 4], in_=turned[:].rearrange("p (c n) -> p c n", c=4)[:, :, ROW])
+                nc.tensor.transpose(turned[h][:, P * c : P * (c + 1)], picked[:, BANK * h + P * c : BANK * h + P * (c + 1)], ident[:])
+            nc.scalar.copy(out=max_cols[:, 4 * h : 4 * h + 4], in_=turned[h][:].rearrange("p (c n) -> p c n", c=4)[:, :, ROW])
 
         picked_scale = keep.tile([P, S], U8, name="picked_scale", align_bytes=64)
         nc.vector.tensor_copy(picked_scale[:, half(0)], scale_table[:].indirect(half_list(0)))
         col_max = keep.tile([P, 1], F32, name="col_max", tag="max_then_codes", align_bytes=64)
-        nc.vector.tensor_reduce(out=col_max[:], in_=max_cols[:], axis=AXIS.X, op=ALU.max)
-        max_row = bank(4)
+        nc.vector.tensor_reduce(out=col_max[:], in_=max_cols[:, : S // P], axis=AXIS.X, op=ALU.max)
+        max_row = bank(3)
         nc.tensor.transpose(max_row[:, :P], col_max[:].to_broadcast([P, P]), ident[:])
+        cols = shared.tile([P, S // P], F32, name="cols", offset=2 * P, align_bytes=64)
+        for h in range(HALVES):
+            nc.scalar.copy(out=cols[:, 4 * h : 4 * h + 4], in_=turned[h][:].rearrange("p (c n) -> p c n", c=4)[:, :, ROW])
         nc.vector.tensor_copy(picked_scale[:, half(1)], scale_table[:].indirect(half_list(1)))
         for r in range(4):
             nc.sync.dma_start(out=x_scale[r:P:32, :].bitcast(I32), in_=picked_scale[8 * r : P : 32, :].bitcast(I32))
         w2_raw.append(load_w2_half(1, "scales_then_w2"))
 
-        def quantize_w1(u, tag):
+        def quantize_w1(u, scales):
             codes = keep.tile([P, 2 * P], U32, name="w1_codes%d" % u, align_bytes=64)
-            scales = keep.tile([P, 2 * P], U8, name="w1_scales%d" % u, tag=tag, align_bytes=64)
             nc.vector.quantize_mx(
                 out=codes[:].bitcast(FP8X4),
                 scales=scales[:],
@@ -128,7 +130,8 @@ def tile_picked_ygcb_relu_po_kernel(tc, x_words, x_scales, w1, w2, score, offs, 
             )
             return codes, scales
 
-        w1_mx = [quantize_w1(0, "w1_scales")]
+        first_scales = shared.tile([P, 2 * P], U8, name="w1_scales0", offset=0, align_bytes=64)
+        w1_mx = [quantize_w1(0, first_scales)]
 
         neg_max = keep.tile([P, 1], F32, name="neg_max", tag="w2_grouped", align_bytes=64)
         nc.vector.tensor_reduce(out=neg_max[:], in_=max_row[:, :P], axis=AXIS.X, op=ALU.max, negate=True)
@@ -149,7 +152,8 @@ def tile_picked_ygcb_relu_po_kernel(tc, x_words, x_scales, w1, w2, score, offs, 
         x_codes = keep.tile([P, S], U32, name="x_codes", tag="max_then_codes", align_bytes=64)
         for h in range(HALVES):
             nc.vector.tensor_copy(x_codes[:, half(h)], word_table[:].bitcast(U32).indirect(half_list(h)))
-        w1_mx.append(quantize_w1(1, "words_then_scales"))
+        last_scales = keep.tile([P, 2 * P], U8, name="w1_scales1", tag="words_then_scales", align_bytes=64)
+        w1_mx.append(quantize_w1(1, last_scales))
 
         def group_weight(raw, label, copies):
             grouped = keep.tile([P, PACK, P, PACK], BF16, name=label + "_grouped", tag=label + "_grouped", align_bytes=64)
@@ -166,7 +170,7 @@ def tile_picked_ygcb_relu_po_kernel(tc, x_words, x_scales, w1, w2, score, offs, 
 
         y = {}
         order = [(t, h) for t in range(PACK) for h in range(HALVES)]
-        for t, h in order:
+        for t, h in [(0, 0), (1, 0), (0, 1), (1, 1)] + order[4:]:
             if True:
                 y[t, h] = bank(HALVES * t + h)
                 nc.tensor.matmul_mx(

@@ -28,6 +28,7 @@ CHUNKS = len(WIDTHS)
 OUT_WIDTHS = (256, 256, 256, 128, 128)
 OUT_STARTS = tuple(sum(OUT_WIDTHS[:c]) for c in range(len(OUT_WIDTHS)))
 QUADS = 4
+AXI = 256
 RUN = 4
 ROW = P - 1
 SLOW_END = 1023
@@ -54,29 +55,29 @@ def tile_picked_ygcb_relu_po_kernel(tc, x_words, x_scales, w1, w2, score, offs, 
         offsets = keep.tile([P, S // 16], U16, name="offsets")
         nc.sync.dma_start(offsets[:], offs)
 
-        scale_table = keep.tile([P, T], U8, name="scale_table", tag="scales_then_w2", align_bytes=64)
+        scale_table = keep.tile([P, T], U8, name="scale_table", tag="scales_then_w2", align_bytes=AXI)
         zero = keep.tile([P, 1], F32, name="zero")
         nc.gpsimd.memset(zero[:], 0.0)
         nc.gpsimd.memset(scale_table[:].bitcast(I32), 0)
-        score_table = keep.tile([P, T], F32, name="score_table")
+        score_table = keep.tile([P, T], F32, name="score_table", align_bytes=AXI)
         nc.vector.memset(score_table[:ROW, :SLOW_END].bitcast(I32), 0)
         nc.vector.memset(score_table[:ROW, SLOW_END:VECTOR_END].bitcast(I32), 0)
         nc.scalar.copy(out=score_table[:ROW, VECTOR_END:], in_=zero[:ROW, :].to_broadcast([ROW, T - VECTOR_END]))
         ident = keep.tile([P, P], F32, name="ident")
         make_identity(nc, ident[:])
-        x_scale = keep.tile([P, S], U8, name="x_scale", align_bytes=64)
+        x_scale = keep.tile([P, S], U8, name="x_scale", align_bytes=AXI)
         nc.gpsimd.memset(x_scale[:].bitcast(I32), 0)
 
         nc.sync.dma_start(out=score_table[ROW:, :], in_=score[0:1, :])
-        w1_raw = keep.tile([P, PACK, H], F32, name="w1_raw")
+        w1_raw = keep.tile([P, PACK, H], F32, name="w1_raw", align_bytes=AXI)
         nc.sync.dma_start(out=w1_raw[:], in_=w1.rearrange("(p j) c -> p j c", j=PACK))
         nc.sync.dma_start(out=scale_table[0:P:8, :].bitcast(I32), in_=x_scales[0].bitcast(I32))
-        word_table = keep.tile([P, T], I32, name="word_table", tag="words_then_scales", align_bytes=64)
+        word_table = keep.tile([P, T], I32, name="word_table", tag="words_then_scales", align_bytes=AXI)
         nc.sync.dma_start(out=word_table[:], in_=x_words[0].rearrange("p c r -> p (c r)").bitcast(I32))
 
 
         def load_w2_half(u, tag):
-            raw = keep.tile([P, PACK, N // 2], F32, name="w2_raw%d" % u, tag=tag, align_bytes=64)
+            raw = keep.tile([P, PACK, N // 2], F32, name="w2_raw%d" % u, tag=tag, align_bytes=AXI)
             nc.sync.dma_start(out=raw[:], in_=w2.rearrange("(p j) c -> p j c", j=PACK)[:, :, u * (N // 2) : (u + 1) * (N // 2)])
             return raw
 
@@ -107,7 +108,7 @@ def tile_picked_ygcb_relu_po_kernel(tc, x_words, x_scales, w1, w2, score, offs, 
                 nc.tensor.transpose(turned[h][:, P * c : P * (c + 1)], picked[:, BANK * h + P * c : BANK * h + P * (c + 1)], ident[:])
             nc.scalar.copy(out=max_cols[:, 4 * h : 4 * h + 4], in_=turned[h][:].rearrange("p (c n) -> p c n", c=4)[:, :, ROW])
 
-        picked_scale = keep.tile([P, S], U8, name="picked_scale", align_bytes=64)
+        picked_scale = keep.tile([P, S], U8, name="picked_scale", align_bytes=AXI)
         nc.vector.tensor_copy(picked_scale[:, half(0)], scale_table[:].indirect(half_list(0)))
         col_max = keep.tile([P, 1], F32, name="col_max", tag="max_then_codes", align_bytes=64)
         nc.vector.tensor_reduce(out=col_max[:], in_=max_cols[:, : S // P], axis=AXIS.X, op=ALU.max)
@@ -152,7 +153,7 @@ def tile_picked_ygcb_relu_po_kernel(tc, x_words, x_scales, w1, w2, score, offs, 
         x_codes = keep.tile([P, S], U32, name="x_codes", tag="max_then_codes", align_bytes=64)
         for h in range(HALVES):
             nc.vector.tensor_copy(x_codes[:, half(h)], word_table[:].bitcast(U32).indirect(half_list(h)))
-        last_scales = keep.tile([P, 2 * P], U8, name="w1_scales1", tag="words_then_scales", align_bytes=64)
+        last_scales = keep.tile([P, 2 * P], U8, name="w1_scales1", tag="words_then_scales", align_bytes=AXI)
         w1_mx.append(quantize_w1(1, last_scales))
 
         def group_weight(raw, label, copies):
@@ -185,7 +186,7 @@ def tile_picked_ygcb_relu_po_kernel(tc, x_words, x_scales, w1, w2, score, offs, 
 
         w2_grouped = group_weight(w2_raw, "w2", (nc.scalar.copy, nc.scalar.copy))
 
-        z_planes = keep.tile([P, PACK, S], BF16, name="z_planes", tag="scales_then_w2", align_bytes=64)
+        z_planes = keep.tile([P, PACK, S], BF16, name="z_planes", tag="scales_then_w2", align_bytes=AXI)
         parts = [keep.tile([P, HALVES], F32, name="part%d" % t) for t in range(PACK)]
 
         def weighted_sum(t, h):
@@ -227,9 +228,9 @@ def tile_picked_ygcb_relu_po_kernel(tc, x_words, x_scales, w1, w2, score, offs, 
 
         out_rows = out_0.rearrange("(p t) j -> p t j", t=PACK)
         out_words = out_1[0].rearrange("p c r -> p (c r)").bitcast(I32)
-        out_codes = keep.tile([P, S], I32, name="out_codes", align_bytes=64)
-        out_scales = keep.tile([P, S // QUADS], U8, name="out_scales", align_bytes=64)
-        result = keep.tile([P, PACK, S], F32, name="result")
+        out_codes = keep.tile([P, S], I32, name="out_codes", align_bytes=AXI)
+        out_scales = keep.tile([P, S // QUADS], U8, name="out_scales", align_bytes=AXI)
+        result = keep.tile([P, PACK, S], F32, name="result", align_bytes=AXI)
         w2_codes = keep.tile([P, PACK * P], U32, name="w2_codes", align_bytes=64)
         w2_scales = keep.tile([P, PACK * P], U8, name="w2_scales", align_bytes=64)
         z_grouped, out_grouped = {}, {}

@@ -100,7 +100,7 @@ def tile_picked_ygcb_relu_po_kernel(tc, x_words, x_scales, w1, w2, score, offs, 
         picked = keep.tile([P, S], F32, name="picked")
         for h in range(HALVES):
             nc.vector.tensor_copy(picked[:, half(h)], score_table[:].indirect(half_list(h)))
-        max_cols = shared.tile([P, P], F32, name="max_cols", offset=0, align_bytes=64)
+        max_cols = shared.tile([P, 2 * P], F32, name="max_cols", offset=0, align_bytes=64)
         turned = []
         for h in range(HALVES):
             turned.append(bank(6 + h))
@@ -114,7 +114,7 @@ def tile_picked_ygcb_relu_po_kernel(tc, x_words, x_scales, w1, w2, score, offs, 
         nc.vector.tensor_reduce(out=col_max[:], in_=max_cols[:, : S // P], axis=AXIS.X, op=ALU.max)
         max_row = bank(3)
         nc.tensor.transpose(max_row[:, :P], col_max[:].to_broadcast([P, P]), ident[:])
-        cols = shared.tile([P, S // P], F32, name="cols", offset=2 * P, align_bytes=64)
+        cols = shared.tile([P, S // P], F32, name="cols", offset=4 * P, align_bytes=64)
         for h in range(HALVES):
             nc.scalar.copy(out=cols[:, 4 * h : 4 * h + 4], in_=turned[h][:].rearrange("p (c n) -> p c n", c=4)[:, :, ROW])
         nc.vector.tensor_copy(picked_scale[:, half(1)], scale_table[:].indirect(half_list(1)))
@@ -122,17 +122,11 @@ def tile_picked_ygcb_relu_po_kernel(tc, x_words, x_scales, w1, w2, score, offs, 
             nc.sync.dma_start(out=x_scale[r:P:32, :].bitcast(I32), in_=picked_scale[8 * r : P : 32, :].bitcast(I32))
         w2_raw.append(load_w2_half(1, "scales_then_w2"))
 
-        def quantize_w1(u, scales):
-            codes = keep.tile([P, 2 * P], U32, name="w1_codes%d" % u, align_bytes=64)
-            nc.vector.quantize_mx(
-                out=codes[:].bitcast(FP8X4),
-                scales=scales[:],
-                in_=w1_grouped[:, 2 * u : 2 * u + 2, :, :].rearrange("p t m j -> p (t m j)"),
-            )
-            return codes, scales
-
-        first_scales = shared.tile([P, 2 * P], U8, name="w1_scales0", offset=0, align_bytes=64)
-        w1_mx = [quantize_w1(0, first_scales)]
+        w1_codes = keep.tile([P, PACK * P], U32, name="w1_codes", align_bytes=64)
+        w1_scales = shared.tile([P, PACK * P], U8, name="w1_scales", offset=0, align_bytes=64)
+        nc.vector.quantize_mx(
+            out=w1_codes[:].bitcast(FP8X4), scales=w1_scales[:], in_=w1_grouped[:].rearrange("p t m j -> p (t m j)")
+        )
 
         neg_max = keep.tile([P, 1], F32, name="neg_max", tag="w2_grouped", align_bytes=64)
         nc.vector.tensor_reduce(out=neg_max[:], in_=max_row[:, :P], axis=AXIS.X, op=ALU.max, negate=True)
@@ -153,8 +147,6 @@ def tile_picked_ygcb_relu_po_kernel(tc, x_words, x_scales, w1, w2, score, offs, 
         x_codes = keep.tile([P, S], U32, name="x_codes", tag="max_then_codes", align_bytes=64)
         for h in range(HALVES):
             nc.vector.tensor_copy(x_codes[:, half(h)], word_table[:].bitcast(U32).indirect(half_list(h)))
-        last_scales = keep.tile([P, 2 * P], U8, name="w1_scales1", tag="words_then_scales", align_bytes=AXI)
-        w1_mx.append(quantize_w1(1, last_scales))
 
         def group_weight(raw, label, copies):
             grouped = keep.tile([P, PACK, P, PACK], BF16, name=label + "_grouped", tag=label + "_grouped", align_bytes=64)
@@ -176,8 +168,8 @@ def tile_picked_ygcb_relu_po_kernel(tc, x_words, x_scales, w1, w2, score, offs, 
                 y[t, h] = bank(HALVES * t + h)
                 nc.tensor.matmul_mx(
                     out=y[t, h][:],
-                    lhsT=w1_mx[t // 2][0][:, P * (t % 2) : P * (t % 2 + 1)].bitcast(FP8X4),
-                    lhsT_scale=w1_mx[t // 2][1][:, P * (t % 2) : P * (t % 2 + 1)],
+                    lhsT=w1_codes[:, P * t : P * (t + 1)].bitcast(FP8X4),
+                    lhsT_scale=w1_scales[:, P * t : P * (t + 1)],
                     rhs=x_codes[:, half(h)].bitcast(FP8X4),
                     rhs_scale=x_scale[:, half(h)],
                     start=True,
@@ -186,7 +178,12 @@ def tile_picked_ygcb_relu_po_kernel(tc, x_words, x_scales, w1, w2, score, offs, 
 
         w2_grouped = group_weight(w2_raw, "w2", (nc.scalar.copy, nc.scalar.copy))
 
-        z_planes = keep.tile([P, PACK, S], BF16, name="z_planes", tag="scales_then_w2", align_bytes=AXI)
+        z_planes = [
+            keep.tile([P, PACK, BANK], BF16, name="z_planes0", tag="scales_then_w2", align_bytes=AXI),
+            keep.tile([P, PACK, BANK], BF16, name="z_planes1", align_bytes=64),
+        ]
+        floor = z_planes[1][:, PACK - 1, 0:2].bitcast(F32)
+        nc.gpsimd.memset(floor, 0.0)
         parts = [keep.tile([P, HALVES], F32, name="part%d" % t) for t in range(PACK)]
 
         def weighted_sum(t, h):
@@ -207,11 +204,15 @@ def tile_picked_ygcb_relu_po_kernel(tc, x_words, x_scales, w1, w2, score, offs, 
             engine.tensor_scalar(
                 out=context[:], in0=parts[t][:, 0:1], scalar1=parts[t][:, 1:2], scalar2=inv_total[:], op0=ALU.add, op1=ALU.mult
             )
-            cuts = STARTS[:5] + (S,) if t == PACK - 1 else (0, BANK, S)
+            if t == PACK - 1:
+                nc.vector.tensor_scalar(
+                    out=z_planes[0][:, t, : STARTS[2]], in0=y[t, 0][:, : STARTS[2]], scalar1=context[:], scalar2=floor, op0=ALU.add, op1=ALU.max
+                )
+            cuts = STARTS[2:5] + (S,) if t == PACK - 1 else (0, BANK, S)
             for c0, c1 in zip(cuts, cuts[1:]):
                 h = c0 // BANK
                 nc.scalar.activation(
-                    out=z_planes[:, t, c0:c1],
+                    out=z_planes[h][:, t, c0 - BANK * h : c1 - BANK * h],
                     in_=y[t, h][:, c0 - BANK * h : c1 - BANK * h],
                     func=ACT.Relu,
                     bias=context[:],
@@ -247,7 +248,7 @@ def tile_picked_ygcb_relu_po_kernel(tc, x_words, x_scales, w1, w2, score, offs, 
 
         def group_z(c):
             z_grouped[c] = keep.tile([P, WIDTHS[c], PACK], BF16, name="z_grouped%d" % c, align_bytes=64)
-            interleave(nc.scalar.copy if c == CHUNKS - 1 else nc.vector.tensor_copy, z_grouped[c][:], z_planes[:, :, chunk(c)])
+            interleave(nc.scalar.copy if c == CHUNKS - 1 else nc.vector.tensor_copy, z_grouped[c][:], z_planes[STARTS[c] // BANK][:, :, STARTS[c] % BANK : STARTS[c] % BANK + WIDTHS[c]])
 
         def second_product(c):
             width = WIDTHS[c]
@@ -304,7 +305,7 @@ def tile_picked_ygcb_relu_po_kernel(tc, x_words, x_scales, w1, w2, score, offs, 
             group_out(c + 1)
             hand_on(c)
         hand_on(len(OUT_WIDTHS) - 1)
-        early = OUT_STARTS[3]
+        early = OUT_STARTS[2]
         nc.sync.dma_start(out=out_words[:, :early], in_=out_codes[:, :early])
         nc.sync.dma_start(out=out_words[:, early:], in_=out_codes[:, early:])
         for q in range(QUADS):

@@ -21,18 +21,28 @@ P = 128
 PACK = 4
 BANK = 512
 HALVES = S // BANK
-WIDTHS = (64, 64, 128, 256, 256, 128, 128)
-FIRST_BANKS = (0, 1, 2, 3, 5, 6, 7)
-STARTS = tuple(sum(WIDTHS[:c]) for c in range(len(WIDTHS)))
-CHUNKS = len(WIDTHS)
-OUT_WIDTHS = (256, 256, 256, 128, 128)
-OUT_STARTS = tuple(sum(OUT_WIDTHS[:c]) for c in range(len(OUT_WIDTHS)))
+BLOCKS = BANK // P
 QUADS = 4
-AXI = 256
+LAST = PACK - 1
+MX_ALIGN = 64
+DMA_ALIGN = 256
 RUN = 4
 ROW = P - 1
-SLOW_END = 1023
+MAX_BANK = 3
+
+ODD_END = 1023
 VECTOR_END = 3583
+
+WIDTHS = (64, 64, 128, 256, 256, 128, 128)
+STARTS = tuple(sum(WIDTHS[:c]) for c in range(len(WIDTHS)))
+CHUNKS = len(WIDTHS)
+CHUNK_BANKS = ((0,), (1,), (2,), (3, 4), (5, 0), (6,), (7,))
+OWN_END = STARTS[2]
+
+OUT_WIDTHS = (256, 256, 256, 128, 128)
+OUT_STARTS = tuple(sum(OUT_WIDTHS[:c]) for c in range(len(OUT_WIDTHS)))
+PIECES = len(OUT_WIDTHS)
+STRIP = S // QUADS
 
 
 def interleave(engine_copy, out, planes):
@@ -40,6 +50,10 @@ def interleave(engine_copy, out, planes):
         out=out.rearrange("p (c i) t -> p c t i", i=RUN),
         in_=planes.rearrange("p t (c i) -> p c t i", i=RUN),
     )
+
+
+def deal_columns(nc, out, raw):
+    nc.scalar.copy(out=out.rearrange("p t m j -> p m j t"), in_=raw.rearrange("p j (m t) -> p m j t", t=PACK))
 
 
 def tile_picked_ygcb_relu_po_kernel(tc, x_words, x_scales, w1, w2, score, offs, out_0, out_1, out_2):
@@ -52,91 +66,104 @@ def tile_picked_ygcb_relu_po_kernel(tc, x_words, x_scales, w1, w2, score, offs, 
         def bank(b):
             return psum.tile([P, BANK], F32, name="bank%d" % b)
 
+        def half(h):
+            return slice(BANK * h, BANK * (h + 1))
+
+        def plane_cols(t):
+            return slice(P * t, P * (t + 1))
+
+        def product(out, w_codes, w_scales, t, codes, scales):
+            nc.tensor.matmul_mx(
+                out=out,
+                lhsT=w_codes[:, plane_cols(t)].bitcast(FP8X4),
+                lhsT_scale=w_scales[:, plane_cols(t)],
+                rhs=codes.bitcast(FP8X4),
+                rhs_scale=scales,
+                start=True,
+                stop=True,
+            )
+
         offsets = keep.tile([P, S // 16], U16, name="offsets")
         nc.sync.dma_start(offsets[:], offs)
 
-        scale_table = keep.tile([P, T], U8, name="scale_table", tag="scales_then_w2", align_bytes=AXI)
+        def half_list(h):
+            return offsets[:, h * (BANK // 16) : (h + 1) * (BANK // 16)]
+
+        scale_table = keep.tile([P, T], U8, name="scale_table", tag="scales_then_w2", align_bytes=DMA_ALIGN)
         zero = keep.tile([P, 1], F32, name="zero")
         nc.gpsimd.memset(zero[:], 0.0)
         nc.gpsimd.memset(scale_table[:].bitcast(I32), 0)
-        score_table = keep.tile([P, T], F32, name="score_table", align_bytes=AXI)
-        nc.vector.memset(score_table[:ROW, :SLOW_END].bitcast(I32), 0)
-        nc.vector.memset(score_table[:ROW, SLOW_END:VECTOR_END].bitcast(I32), 0)
+        score_table = keep.tile([P, T], F32, name="score_table", align_bytes=DMA_ALIGN)
+        nc.vector.memset(score_table[:ROW, :ODD_END].bitcast(I32), 0)
+        nc.vector.memset(score_table[:ROW, ODD_END:VECTOR_END].bitcast(I32), 0)
         nc.scalar.copy(out=score_table[:ROW, VECTOR_END:], in_=zero[:ROW, :].to_broadcast([ROW, T - VECTOR_END]))
         ident = keep.tile([P, P], F32, name="ident")
         make_identity(nc, ident[:])
-        x_scale = keep.tile([P, S], U8, name="x_scale", align_bytes=AXI)
+        x_scale = keep.tile([P, S], U8, name="x_scale", align_bytes=DMA_ALIGN)
         nc.gpsimd.memset(x_scale[:].bitcast(I32), 0)
 
         nc.sync.dma_start(out=score_table[ROW:, :], in_=score[0:1, :])
-        w1_raw = keep.tile([P, PACK, H], F32, name="w1_raw", align_bytes=AXI)
+        w1_raw = keep.tile([P, PACK, H], F32, name="w1_raw", align_bytes=DMA_ALIGN)
         nc.sync.dma_start(out=w1_raw[:], in_=w1.rearrange("(p j) c -> p j c", j=PACK))
         nc.sync.dma_start(out=scale_table[0:P:8, :].bitcast(I32), in_=x_scales[0].bitcast(I32))
-        word_table = keep.tile([P, T], I32, name="word_table", tag="words_then_scales", align_bytes=AXI)
+        word_table = keep.tile([P, T], I32, name="word_table", align_bytes=DMA_ALIGN)
         nc.sync.dma_start(out=word_table[:], in_=x_words[0].rearrange("p c r -> p (c r)").bitcast(I32))
 
-
         def load_w2_half(u, tag):
-            raw = keep.tile([P, PACK, N // 2], F32, name="w2_raw%d" % u, tag=tag, align_bytes=AXI)
+            raw = keep.tile([P, PACK, N // 2], F32, name="w2_raw%d" % u, tag=tag, align_bytes=DMA_ALIGN)
             nc.sync.dma_start(out=raw[:], in_=w2.rearrange("(p j) c -> p j c", j=PACK)[:, :, u * (N // 2) : (u + 1) * (N // 2)])
             return raw
 
         w2_raw = [load_w2_half(0, "w2_first_half")]
 
-        warm = keep.tile([P, 1], F32, name="warm")
-        nc.scalar.activation(out=warm[:], in_=zero[:], func=ACT.Exp)
-
-        def half(h):
-            return slice(BANK * h, BANK * (h + 1))
-
-        def half_list(h):
-            return offsets[:, h * (BANK // 16) : (h + 1) * (BANK // 16)]
-
-        w1_grouped = keep.tile([P, PACK, P, PACK], BF16, name="w1_grouped", align_bytes=64)
-        nc.scalar.copy(
-            out=w1_grouped[:].rearrange("p t m j -> p m j t"), in_=w1_raw[:].rearrange("p j (m t) -> p m j t", t=PACK)
-        )
+        w1_grouped = keep.tile([P, PACK, P, PACK], BF16, name="w1_grouped", align_bytes=MX_ALIGN)
+        deal_columns(nc, w1_grouped[:], w1_raw[:])
 
         picked = keep.tile([P, S], F32, name="picked")
         for h in range(HALVES):
             nc.vector.tensor_copy(picked[:, half(h)], score_table[:].indirect(half_list(h)))
-        max_cols = shared.tile([P, 2 * P], F32, name="max_cols", offset=0, align_bytes=64)
+        max_cols = shared.tile([P, 2 * P], F32, name="max_cols", offset=0, align_bytes=MX_ALIGN)
         turned = []
-        for h in range(HALVES):
-            turned.append(bank(6 + h))
-            for c in range(4):
-                nc.tensor.transpose(turned[h][:, P * c : P * (c + 1)], picked[:, BANK * h + P * c : BANK * h + P * (c + 1)], ident[:])
-            nc.scalar.copy(out=max_cols[:, 4 * h : 4 * h + 4], in_=turned[h][:].rearrange("p (c n) -> p c n", c=4)[:, :, ROW])
 
-        picked_scale = keep.tile([P, S], U8, name="picked_scale", align_bytes=AXI)
-        nc.vector.tensor_copy(picked_scale[:, half(0)], scale_table[:].indirect(half_list(0)))
-        col_max = keep.tile([P, 1], F32, name="col_max", tag="max_then_codes", align_bytes=64)
-        nc.vector.tensor_reduce(out=col_max[:], in_=max_cols[:, : S // P], axis=AXIS.X, op=ALU.max)
-        max_row = bank(3)
-        nc.tensor.transpose(max_row[:, :P], col_max[:].to_broadcast([P, P]), ident[:])
-        cols = shared.tile([P, S // P], F32, name="cols", offset=4 * P, align_bytes=64)
+        def take_columns(out, h):
+            nc.scalar.copy(
+                out=out[:, BLOCKS * h : BLOCKS * (h + 1)], in_=turned[h][:].rearrange("p (c n) -> p c n", c=BLOCKS)[:, :, ROW]
+            )
+
         for h in range(HALVES):
-            nc.scalar.copy(out=cols[:, 4 * h : 4 * h + 4], in_=turned[h][:].rearrange("p (c n) -> p c n", c=4)[:, :, ROW])
+            turned.append(bank(HALVES * LAST + h))
+            for c in range(BLOCKS):
+                nc.tensor.transpose(turned[h][:, plane_cols(c)], picked[:, BANK * h + P * c : BANK * h + P * (c + 1)], ident[:])
+            take_columns(max_cols, h)
+
+        picked_scale = keep.tile([P, S], U8, name="picked_scale", align_bytes=DMA_ALIGN)
+        nc.vector.tensor_copy(picked_scale[:, half(0)], scale_table[:].indirect(half_list(0)))
+        col_max = keep.tile([P, 1], F32, name="col_max", tag="max_then_codes", align_bytes=MX_ALIGN)
+        nc.vector.tensor_reduce(out=col_max[:], in_=max_cols[:, : S // P], axis=AXIS.X, op=ALU.max)
+        max_row = bank(MAX_BANK)
+        nc.tensor.transpose(max_row[:, :P], col_max[:].to_broadcast([P, P]), ident[:])
+        cols = shared.tile([P, S // P], F32, name="cols", offset=PACK * P, align_bytes=MX_ALIGN)
+        for h in range(HALVES):
+            take_columns(cols, h)
         nc.vector.tensor_copy(picked_scale[:, half(1)], scale_table[:].indirect(half_list(1)))
-        for r in range(4):
+        for r in range(PACK):
             nc.sync.dma_start(out=x_scale[r:P:32, :].bitcast(I32), in_=picked_scale[8 * r : P : 32, :].bitcast(I32))
         w2_raw.append(load_w2_half(1, "scales_then_w2"))
 
-        w1_codes = keep.tile([P, PACK * P], U32, name="w1_codes", align_bytes=64)
-        w1_scales = shared.tile([P, PACK * P], U8, name="w1_scales", offset=0, align_bytes=64)
+        w1_codes = keep.tile([P, PACK * P], U32, name="w1_codes", align_bytes=MX_ALIGN)
+        w1_scales = shared.tile([P, PACK * P], U8, name="w1_scales", offset=0, align_bytes=MX_ALIGN)
         nc.vector.quantize_mx(
             out=w1_codes[:].bitcast(FP8X4), scales=w1_scales[:], in_=w1_grouped[:].rearrange("p t m j -> p (t m j)")
         )
 
-        neg_max = keep.tile([P, 1], F32, name="neg_max", tag="w2_grouped", align_bytes=64)
+        neg_max = keep.tile([P, 1], F32, name="neg_max", tag="w2_grouped", align_bytes=MX_ALIGN)
         nc.vector.tensor_reduce(out=neg_max[:], in_=max_row[:, :P], axis=AXIS.X, op=ALU.max, negate=True)
         spread = []
         for h in range(HALVES):
-            spread.append(bank(4 + h))
-            for c in range(4):
-                nc.tensor.transpose(
-                    spread[h][:, P * c : P * (c + 1)], cols[:, 4 * h + c : 4 * h + c + 1].to_broadcast([P, P]), ident[:]
-                )
+            spread.append(bank(HALVES * (LAST - 1) + h))
+            for c in range(BLOCKS):
+                column = cols[:, BLOCKS * h + c : BLOCKS * h + c + 1]
+                nc.tensor.transpose(spread[h][:, plane_cols(c)], column.to_broadcast([P, P]), ident[:])
         weights = keep.tile([P, S], F32, name="weights")
         totals = keep.tile([P, HALVES], F32, name="totals")
         for h in range(HALVES):
@@ -144,45 +171,28 @@ def tile_picked_ygcb_relu_po_kernel(tc, x_words, x_scales, w1, w2, score, offs, 
                 out=weights[:, half(h)], in_=spread[h][:], func=ACT.Exp, bias=neg_max[:], scale=1.0, accum_out=totals[:, h : h + 1]
             )
 
-        x_codes = keep.tile([P, S], U32, name="x_codes", tag="max_then_codes", align_bytes=64)
+        x_codes = keep.tile([P, S], U32, name="x_codes", tag="max_then_codes", align_bytes=MX_ALIGN)
         for h in range(HALVES):
             nc.vector.tensor_copy(x_codes[:, half(h)], word_table[:].bitcast(U32).indirect(half_list(h)))
-
-        def group_weight(raw, label, copies):
-            grouped = keep.tile([P, PACK, P, PACK], BF16, name=label + "_grouped", tag=label + "_grouped", align_bytes=64)
-            for u in range(2):
-                copies[u](
-                    out=grouped[:, :, u * (P // 2) : (u + 1) * (P // 2), :].rearrange("p t m j -> p m j t"),
-                    in_=raw[u][:].rearrange("p j (m t) -> p m j t", t=PACK),
-                )
-            return grouped
-
 
         total = keep.tile([P, 1], F32, name="total")
         nc.gpsimd.tensor_tensor(out=total[:], in0=totals[:, 0:1], in1=totals[:, 1:2], op=ALU.add)
 
         y = {}
         order = [(t, h) for t in range(PACK) for h in range(HALVES)]
-        for t, h in [(0, 0), (1, 0), (0, 1), (1, 1)] + order[4:]:
-            if True:
-                y[t, h] = bank(HALVES * t + h)
-                nc.tensor.matmul_mx(
-                    out=y[t, h][:],
-                    lhsT=w1_codes[:, P * t : P * (t + 1)].bitcast(FP8X4),
-                    lhsT_scale=w1_scales[:, P * t : P * (t + 1)],
-                    rhs=x_codes[:, half(h)].bitcast(FP8X4),
-                    rhs_scale=x_scale[:, half(h)],
-                    start=True,
-                    stop=True,
-                )
+        for t, h in [(t, h) for h in range(HALVES) for t in range(2)] + order[2 * HALVES :]:
+            y[t, h] = bank(HALVES * t + h)
+            product(y[t, h][:], w1_codes, w1_scales, t, x_codes[:, half(h)], x_scale[:, half(h)])
 
-        w2_grouped = group_weight(w2_raw, "w2", (nc.scalar.copy, nc.scalar.copy))
+        w2_grouped = keep.tile([P, PACK, P, PACK], BF16, name="w2_grouped", tag="w2_grouped", align_bytes=MX_ALIGN)
+        for u in range(2):
+            deal_columns(nc, w2_grouped[:, :, u * (P // 2) : (u + 1) * (P // 2), :], w2_raw[u][:])
 
         z_planes = [
-            keep.tile([P, PACK, BANK], BF16, name="z_planes0", tag="scales_then_w2", align_bytes=AXI),
-            keep.tile([P, PACK, BANK], BF16, name="z_planes1", align_bytes=64),
+            keep.tile([P, PACK, BANK], BF16, name="z_planes0", tag="scales_then_w2", align_bytes=DMA_ALIGN),
+            keep.tile([P, PACK, BANK], BF16, name="z_planes1", align_bytes=MX_ALIGN),
         ]
-        floor = z_planes[1][:, PACK - 1, 0:2].bitcast(F32)
+        floor = z_planes[1][:, LAST, 0:2].bitcast(F32)
         nc.gpsimd.memset(floor, 0.0)
         parts = [keep.tile([P, HALVES], F32, name="part%d" % t) for t in range(PACK)]
 
@@ -200,15 +210,16 @@ def tile_picked_ygcb_relu_po_kernel(tc, x_words, x_scales, w1, w2, score, offs, 
 
         def add_context(t):
             context = keep.tile([P, 1], F32, name="context%d" % t)
-            engine = nc.vector if t == PACK - 1 else nc.gpsimd
+            engine = nc.vector if t == LAST else nc.gpsimd
             engine.tensor_scalar(
                 out=context[:], in0=parts[t][:, 0:1], scalar1=parts[t][:, 1:2], scalar2=inv_total[:], op0=ALU.add, op1=ALU.mult
             )
-            if t == PACK - 1:
+            cuts = (0, BANK, S)
+            if t == LAST:
                 nc.vector.tensor_scalar(
-                    out=z_planes[0][:, t, : STARTS[2]], in0=y[t, 0][:, : STARTS[2]], scalar1=context[:], scalar2=floor, op0=ALU.add, op1=ALU.max
+                    out=z_planes[0][:, t, :OWN_END], in0=y[t, 0][:, :OWN_END], scalar1=context[:], scalar2=floor, op0=ALU.add, op1=ALU.max
                 )
-            cuts = STARTS[2:5] + (S,) if t == PACK - 1 else (0, BANK, S)
+                cuts = tuple(c0 for c0 in STARTS if OWN_END <= c0 <= BANK) + (S,)
             for c0, c1 in zip(cuts, cuts[1:]):
                 h = c0 // BANK
                 nc.scalar.activation(
@@ -229,70 +240,70 @@ def tile_picked_ygcb_relu_po_kernel(tc, x_words, x_scales, w1, w2, score, offs, 
 
         out_rows = out_0.rearrange("(p t) j -> p t j", t=PACK)
         out_words = out_1[0].rearrange("p c r -> p (c r)").bitcast(I32)
-        out_codes = keep.tile([P, S], I32, name="out_codes", align_bytes=AXI)
-        out_scales = keep.tile([P, S // QUADS], U8, name="out_scales", align_bytes=AXI)
-        result = keep.tile([P, PACK, S], F32, name="result", align_bytes=AXI)
-        w2_codes = keep.tile([P, PACK * P], U32, name="w2_codes", align_bytes=64)
-        w2_scales = keep.tile([P, PACK * P], U8, name="w2_scales", align_bytes=64)
+        out_codes = keep.tile([P, S], I32, name="out_codes", align_bytes=DMA_ALIGN)
+        out_scales = keep.tile([P, STRIP], U8, name="out_scales", align_bytes=DMA_ALIGN)
+        result = keep.tile([P, PACK, S], F32, name="result", align_bytes=DMA_ALIGN)
+        w2_codes = keep.tile([P, PACK * P], U32, name="w2_codes", align_bytes=MX_ALIGN)
+        w2_scales = keep.tile([P, PACK * P], U8, name="w2_scales", align_bytes=MX_ALIGN)
         z_grouped, out_grouped = {}, {}
 
         def chunk(c):
             return slice(STARTS[c], STARTS[c] + WIDTHS[c])
 
-        def quantize_w2(u):
+        def quantize_w2(t):
             nc.vector.quantize_mx(
-                out=w2_codes[:, 2 * P * u : 2 * P * (u + 1)].bitcast(FP8X4),
-                scales=w2_scales[:, 2 * P * u : 2 * P * (u + 1)],
-                in_=w2_grouped[:, 2 * u : 2 * u + 2, :, :].rearrange("p t m j -> p (t m j)"),
+                out=w2_codes[:, plane_cols(t)].bitcast(FP8X4),
+                scales=w2_scales[:, plane_cols(t)],
+                in_=w2_grouped[:, t, :, :].rearrange("p m j -> p (m j)"),
             )
 
         def group_z(c):
-            z_grouped[c] = keep.tile([P, WIDTHS[c], PACK], BF16, name="z_grouped%d" % c, align_bytes=64)
-            interleave(nc.scalar.copy if c == CHUNKS - 1 else nc.vector.tensor_copy, z_grouped[c][:], z_planes[STARTS[c] // BANK][:, :, STARTS[c] % BANK : STARTS[c] % BANK + WIDTHS[c]])
+            z_grouped[c] = keep.tile([P, WIDTHS[c], PACK], BF16, name="z_grouped%d" % c, align_bytes=MX_ALIGN)
+            h, c0 = divmod(STARTS[c], BANK)
+            copy = nc.scalar.copy if c == CHUNKS - 1 else nc.vector.tensor_copy
+            interleave(copy, z_grouped[c][:], z_planes[h][:, :, c0 : c0 + WIDTHS[c]])
 
         def second_product(c):
             width = WIDTHS[c]
-            z_codes = keep.tile([P, width], U32, name="z_codes%d" % c, align_bytes=64)
-            z_scales = keep.tile([P, width], U8, name="z_scales%d" % c, align_bytes=64)
+            z_codes = keep.tile([P, width], U32, name="z_codes%d" % c, align_bytes=MX_ALIGN)
+            z_scales = keep.tile([P, width], U8, name="z_scales%d" % c, align_bytes=MX_ALIGN)
             nc.vector.quantize_mx(
                 out=z_codes[:].bitcast(FP8X4), scales=z_scales[:], in_=z_grouped[c][:].rearrange("p c t -> p (c t)")
             )
-            per_bank = min(PACK, BANK // width)
-            for t0 in range(0, PACK, per_bank):
-                acc = bank((FIRST_BANKS[c] + t0 // per_bank) % 6 if width == 256 else FIRST_BANKS[c])
+            per_bank = PACK // len(CHUNK_BANKS[c])
+            for n, b in enumerate(CHUNK_BANKS[c]):
+                acc = bank(b)
+                t0 = n * per_bank
                 for v in range(per_bank):
-                    t = t0 + v
-                    nc.tensor.matmul_mx(
-                        out=acc[:, width * v : width * (v + 1)],
-                        lhsT=w2_codes[:, P * t : P * (t + 1)].bitcast(FP8X4),
-                        lhsT_scale=w2_scales[:, P * t : P * (t + 1)],
-                        rhs=z_codes[:].bitcast(FP8X4),
-                        rhs_scale=z_scales[:],
-                        start=True,
-                        stop=True,
-                    )
-                nc.scalar.copy(out=result[:, t0 : t0 + per_bank, chunk(c)], in_=acc[:, : per_bank * width].rearrange("p (t c) -> p t c", t=per_bank))
+                    product(acc[:, width * v : width * (v + 1)], w2_codes, w2_scales, t0 + v, z_codes[:], z_scales[:])
+                nc.scalar.copy(
+                    out=result[:, t0 : t0 + per_bank, chunk(c)],
+                    in_=acc[:, : per_bank * width].rearrange("p (t c) -> p t c", t=per_bank),
+                )
             nc.sync.dma_start(out=out_rows[:, :, chunk(c)], in_=result[:, :, chunk(c)])
 
-        def out_chunk(c):
+        def piece(c):
             return slice(OUT_STARTS[c], OUT_STARTS[c] + OUT_WIDTHS[c])
 
         def group_out(c):
-            out_grouped[c] = keep.tile([P, OUT_WIDTHS[c], PACK], BF16, name="out_grouped%d" % c, align_bytes=64)
-            interleave(nc.scalar.copy if c == len(OUT_WIDTHS) - 1 else nc.vector.tensor_copy, out_grouped[c][:], result[:, :, out_chunk(c)])
+            out_grouped[c] = keep.tile([P, OUT_WIDTHS[c], PACK], BF16, name="out_grouped%d" % c, align_bytes=MX_ALIGN)
+            copy = nc.scalar.copy if c == PIECES - 1 else nc.vector.tensor_copy
+            interleave(copy, out_grouped[c][:], result[:, :, piece(c)])
 
         def hand_on(c):
-            plane, first = divmod(OUT_STARTS[c], S // QUADS)
-            nc.vector.quantize_mx(
-                out=out_codes[:, out_chunk(c)].bitcast(FP8X4),
-                scales=out_scales[4 * plane :, first : first + OUT_WIDTHS[c]],
-                in_=out_grouped[c][:].rearrange("p c t -> p (c t)"),
-            )
+            strip, first = divmod(OUT_STARTS[c], STRIP)
+            step = P if strip >= QUADS - 2 else OUT_WIDTHS[c]
+            for c0 in range(0, OUT_WIDTHS[c], step):
+                nc.vector.quantize_mx(
+                    out=out_codes[:, OUT_STARTS[c] + c0 : OUT_STARTS[c] + c0 + step].bitcast(FP8X4),
+                    scales=out_scales[4 * strip :, first + c0 : first + c0 + step],
+                    in_=out_grouped[c][:, c0 : c0 + step, :].rearrange("p c t -> p (c t)"),
+                )
 
         group_z(CHUNKS - 1)
-        quantize_w2(0)
         group_z(0)
-        quantize_w2(1)
+        for t in range(PACK):
+            quantize_w2(t)
         second_product(0)
         group_z(1)
         for c in range(1, CHUNKS - 2):
@@ -301,13 +312,13 @@ def tile_picked_ygcb_relu_po_kernel(tc, x_words, x_scales, w1, w2, score, offs, 
         second_product(CHUNKS - 2)
         second_product(CHUNKS - 1)
         group_out(0)
-        for c in range(len(OUT_WIDTHS) - 1):
+        for c in range(PIECES - 1):
             group_out(c + 1)
             hand_on(c)
-        hand_on(len(OUT_WIDTHS) - 1)
-        early = OUT_STARTS[2]
-        nc.sync.dma_start(out=out_words[:, :early], in_=out_codes[:, :early])
-        nc.sync.dma_start(out=out_words[:, early:], in_=out_codes[:, early:])
+        hand_on(PIECES - 1)
+
+        for h in range(HALVES):
+            nc.sync.dma_start(out=out_words[:, half(h)], in_=out_codes[:, half(h)])
         for q in range(QUADS):
             queue = nc.sync if q % 2 == 0 else nc.scalar
             queue.dma_start(

@@ -33,13 +33,13 @@ MAX_BANK = 3
 ODD_END = 1023
 VECTOR_END = 3583
 
-WIDTHS = (64, 64, 128, 256, 256, 128, 128)
+WIDTHS = (64, 64, 128, 256, 128, 256, 128)
 STARTS = tuple(sum(WIDTHS[:c]) for c in range(len(WIDTHS)))
 CHUNKS = len(WIDTHS)
-CHUNK_BANKS = ((0,), (1,), (2,), (3, 4), (5, 0), (6,), (7,))
+CHUNK_BANKS = ((0,), (1,), (2,), (3, 4), (5,), (0, 6), (7,))
 OWN_END = STARTS[2]
 
-OUT_WIDTHS = (256, 256, 256, 128, 128)
+OUT_WIDTHS = (256, 256, 128, 256, 128)
 OUT_STARTS = tuple(sum(OUT_WIDTHS[:c]) for c in range(len(OUT_WIDTHS)))
 PIECES = len(OUT_WIDTHS)
 STRIP = S // QUADS
@@ -260,8 +260,7 @@ def tile_picked_ygcb_relu_po_kernel(tc, x_words, x_scales, w1, w2, score, offs, 
         def group_z(c):
             z_grouped[c] = keep.tile([P, WIDTHS[c], PACK], BF16, name="z_grouped%d" % c, align_bytes=MX_ALIGN)
             h, c0 = divmod(STARTS[c], BANK)
-            copy = nc.scalar.copy if c == CHUNKS - 1 else nc.vector.tensor_copy
-            interleave(copy, z_grouped[c][:], z_planes[h][:, :, c0 : c0 + WIDTHS[c]])
+            interleave(nc.vector.tensor_copy, z_grouped[c][:], z_planes[h][:, :, c0 : c0 + WIDTHS[c]])
 
         def second_product(c):
             width = WIDTHS[c]
@@ -291,25 +290,23 @@ def tile_picked_ygcb_relu_po_kernel(tc, x_words, x_scales, w1, w2, score, offs, 
             interleave(copy, out_grouped[c][:], result[:, :, piece(c)])
 
         def hand_on(c):
-            strip, first = divmod(OUT_STARTS[c], STRIP)
-            step = P if strip >= QUADS - 2 else OUT_WIDTHS[c]
+            step = P if OUT_STARTS[c] >= BANK else OUT_WIDTHS[c]
             for c0 in range(0, OUT_WIDTHS[c], step):
+                strip, first = divmod(OUT_STARTS[c] + c0, STRIP)
                 nc.vector.quantize_mx(
                     out=out_codes[:, OUT_STARTS[c] + c0 : OUT_STARTS[c] + c0 + step].bitcast(FP8X4),
-                    scales=out_scales[4 * strip :, first + c0 : first + c0 + step],
+                    scales=out_scales[4 * strip :, first : first + step],
                     in_=out_grouped[c][:, c0 : c0 + step, :].rearrange("p c t -> p (c t)"),
                 )
 
-        group_z(CHUNKS - 1)
         group_z(0)
         for t in range(PACK):
             quantize_w2(t)
         second_product(0)
         group_z(1)
-        for c in range(1, CHUNKS - 2):
+        for c in range(1, CHUNKS - 1):
             group_z(c + 1)
             second_product(c)
-        second_product(CHUNKS - 2)
         second_product(CHUNKS - 1)
         group_out(0)
         for c in range(PIECES - 1):
@@ -317,8 +314,8 @@ def tile_picked_ygcb_relu_po_kernel(tc, x_words, x_scales, w1, w2, score, offs, 
             hand_on(c)
         hand_on(PIECES - 1)
 
-        for h in range(HALVES):
-            nc.sync.dma_start(out=out_words[:, half(h)], in_=out_codes[:, half(h)])
+        for cols in (slice(0, OUT_STARTS[3]), slice(OUT_STARTS[3], S)):
+            nc.sync.dma_start(out=out_words[:, cols], in_=out_codes[:, cols])
         for q in range(QUADS):
             queue = nc.sync if q % 2 == 0 else nc.scalar
             queue.dma_start(

@@ -229,6 +229,8 @@ def tile_picked_ygcb_relu_po_kernel(tc, x_words, x_scales, w1, w2, score, offs, 
                     bias=context[:],
                     scale=1.0,
                 )
+                if t in (1, 2):
+                    product(bank(HALVES * t + h)[:], w1_codes, w1_scales, t, x_codes[:, half(h)], x_scale[:, half(h)])
 
         weighted_sum(*order[0])
         inv_total = keep.tile([P, 1], F32, name="inv_total", tag="weighted0_0")

@@ -120,8 +120,7 @@ def tile_picked_ygcb_relu_po_kernel(tc, x_words, x_scales, w1, w2, score, offs, 
         deal_columns(nc, w1_grouped[:], w1_raw[:])
 
         picked = keep.tile([P, S], F32, name="picked")
-        for h in range(HALVES):
-            nc.vector.tensor_copy(picked[:, half(h)], score_table[:].indirect(half_list(h)))
+        nc.vector.tensor_copy(picked[:], score_table[:].indirect(offsets[:]))
         max_cols = shared.tile([P, 2 * P], F32, name="max_cols", offset=0, align_bytes=MX_ALIGN)
         turned = []
 
@@ -137,7 +136,7 @@ def tile_picked_ygcb_relu_po_kernel(tc, x_words, x_scales, w1, w2, score, offs, 
             take_columns(max_cols, h)
 
         picked_scale = keep.tile([P, S], U8, name="picked_scale", align_bytes=DMA_ALIGN)
-        nc.vector.tensor_copy(picked_scale[:, half(0)], scale_table[:].indirect(half_list(0)))
+        nc.vector.tensor_copy(picked_scale[:], scale_table[:].indirect(offsets[:]))
         col_max = keep.tile([P, 1], F32, name="col_max", tag="max_then_codes", align_bytes=MX_ALIGN)
         nc.vector.tensor_reduce(out=col_max[:], in_=max_cols[:, : S // P], axis=AXIS.X, op=ALU.max)
         max_row = bank(MAX_BANK)
@@ -145,7 +144,6 @@ def tile_picked_ygcb_relu_po_kernel(tc, x_words, x_scales, w1, w2, score, offs, 
         cols = shared.tile([P, S // P], F32, name="cols", offset=PACK * P, align_bytes=MX_ALIGN)
         for h in range(HALVES):
             take_columns(cols, h)
-        nc.vector.tensor_copy(picked_scale[:, half(1)], scale_table[:].indirect(half_list(1)))
         for r in range(PACK):
             nc.sync.dma_start(out=x_scale[r:P:32, :].bitcast(I32), in_=picked_scale[8 * r : P : 32, :].bitcast(I32))
         w2_raw.append(load_w2_half(1, "scales_then_w2"))
@@ -281,7 +279,7 @@ def tile_picked_ygcb_relu_po_kernel(tc, x_words, x_scales, w1, w2, score, offs, 
                     out=result[:, t0 : t0 + per_bank, chunk(c)],
                     in_=acc[:, : per_bank * width].rearrange("p (t c) -> p t c", t=per_bank),
                 )
-            nc.sync.dma_start(out=out_rows[:, :, chunk(c)], in_=result[:, :, chunk(c)])
+                nc.sync.dma_start(out=out_rows[:, t0 : t0 + per_bank, chunk(c)], in_=result[:, t0 : t0 + per_bank, chunk(c)])
 
         def piece(c):
             return slice(OUT_STARTS[c], OUT_STARTS[c] + OUT_WIDTHS[c])

@@ -117,10 +117,11 @@ def tile_picked_ygcb_relu_po_kernel(tc, x_words, x_scales, w1, w2, score, offs, 
         w2_raw = [load_w2_half(0, "w2_first_half")]
 
         w1_grouped = keep.tile([P, PACK, P, PACK], BF16, name="w1_grouped", align_bytes=MX_ALIGN)
-        deal_columns(nc, w1_grouped[:], w1_raw[:])
+        nc.vector.tensor_copy(out=w1_grouped[:].rearrange("p t m j -> p m t j"), in_=w1_raw[:].rearrange("p j (m t) -> p m t j", t=PACK))
 
         picked = keep.tile([P, S], F32, name="picked")
-        nc.vector.tensor_copy(picked[:], score_table[:].indirect(offsets[:]))
+        for h in range(HALVES):
+            nc.scalar.activation(out=picked[:, half(h)], in_=score_table[:].indirect(half_list(h)), func=ACT.Copy)
         max_cols = shared.tile([P, 2 * P], F32, name="max_cols", offset=0, align_bytes=MX_ALIGN)
         turned = []
 
@@ -227,8 +228,6 @@ def tile_picked_ygcb_relu_po_kernel(tc, x_words, x_scales, w1, w2, score, offs, 
                     bias=context[:],
                     scale=1.0,
                 )
-                if t in (1, 2):
-                    product(bank(HALVES * t + h)[:], w1_codes, w1_scales, t, x_codes[:, half(h)], x_scale[:, half(h)])
 
         weighted_sum(*order[0])
         inv_total = keep.tile([P, 1], F32, name="inv_total", tag="weighted0_0")

@@ -30,8 +30,8 @@ RUN = 4
 ROW = P - 1
 MAX_BANK = 3
 
-ODD_END = 1023
-VECTOR_END = 3583
+VECTOR_END = 2383
+SCALAR_END = 2896
 
 WIDTHS = (64, 64, 128, 256, 128, 256, 128)
 STARTS = tuple(sum(WIDTHS[:c]) for c in range(len(WIDTHS)))
@@ -94,9 +94,11 @@ def tile_picked_ygcb_relu_po_kernel(tc, x_words, x_scales, w1, w2, score, offs, 
         nc.gpsimd.memset(zero[:], 0.0)
         nc.gpsimd.memset(scale_table[:].bitcast(I32), 0)
         score_table = keep.tile([P, T], F32, name="score_table", align_bytes=DMA_ALIGN)
-        nc.vector.memset(score_table[:ROW, :ODD_END].bitcast(I32), 0)
-        nc.vector.memset(score_table[:ROW, ODD_END:VECTOR_END].bitcast(I32), 0)
-        nc.scalar.copy(out=score_table[:ROW, VECTOR_END:], in_=zero[:ROW, :].to_broadcast([ROW, T - VECTOR_END]))
+        nc.vector.memset(score_table[:ROW, :VECTOR_END].bitcast(I32), 0)
+        nc.scalar.copy(
+            out=score_table[:ROW, VECTOR_END:SCALAR_END], in_=zero[:ROW, :].to_broadcast([ROW, SCALAR_END - VECTOR_END])
+        )
+        nc.gpsimd.memset(score_table[:ROW, SCALAR_END:].bitcast(I32), 0)
         ident = keep.tile([P, P], F32, name="ident")
         make_identity(nc, ident[:])
         x_scale = keep.tile([P, S], U8, name="x_scale", align_bytes=DMA_ALIGN)
@@ -116,10 +118,7 @@ def tile_picked_ygcb_relu_po_kernel(tc, x_words, x_scales, w1, w2, score, offs, 
 
         w2_raw = [load_w2_half(0, "w2_first_half")]
 
-        w1_grouped = keep.tile([P, PACK, P, PACK], BF16, name="w1_grouped", align_bytes=MX_ALIGN)
-        nc.vector.tensor_copy(out=w1_grouped[:].rearrange("p t m j -> p m t j"), in_=w1_raw[:].rearrange("p j (m t) -> p m t j", t=PACK))
-
-        picked = keep.tile([P, S], F32, name="picked")
+        picked = keep.tile([P, S], F32, name="picked", tag="picked_then_w1", align_bytes=DMA_ALIGN)
         for h in range(HALVES):
             nc.scalar.activation(out=picked[:, half(h)], in_=score_table[:].indirect(half_list(h)), func=ACT.Copy)
         max_cols = shared.tile([P, 2 * P], F32, name="max_cols", offset=0, align_bytes=MX_ALIGN)
@@ -138,6 +137,17 @@ def tile_picked_ygcb_relu_po_kernel(tc, x_words, x_scales, w1, w2, score, offs, 
 
         picked_scale = keep.tile([P, S], U8, name="picked_scale", align_bytes=DMA_ALIGN)
         nc.vector.tensor_copy(picked_scale[:], scale_table[:].indirect(offsets[:]))
+        w1_grouped = []
+
+        def cast_w1(u, copy, tag):
+            w1_grouped.append(keep.tile([P, 2, P, PACK], BF16, name="w1_grouped%d" % u, tag=tag, align_bytes=DMA_ALIGN))
+            copy(
+                out=w1_grouped[u][:].rearrange("p t m j -> p m t j"),
+                in_=w1_raw[:].rearrange("p j (m t) -> p m t j", t=PACK)[:, :, 2 * u : 2 * u + 2],
+            )
+
+        cast_w1(0, nc.vector.tensor_copy, "w1_first_planes")
+        cast_w1(1, nc.scalar.copy, "picked_then_w1")
         col_max = keep.tile([P, 1], F32, name="col_max", tag="max_then_codes", align_bytes=MX_ALIGN)
         nc.vector.tensor_reduce(out=col_max[:], in_=max_cols[:, : S // P], axis=AXIS.X, op=ALU.max)
         max_row = bank(MAX_BANK)
@@ -151,9 +161,13 @@ def tile_picked_ygcb_relu_po_kernel(tc, x_words, x_scales, w1, w2, score, offs, 
 
         w1_codes = keep.tile([P, PACK * P], U32, name="w1_codes", align_bytes=MX_ALIGN)
         w1_scales = shared.tile([P, PACK * P], U8, name="w1_scales", offset=0, align_bytes=MX_ALIGN)
-        nc.vector.quantize_mx(
-            out=w1_codes[:].bitcast(FP8X4), scales=w1_scales[:], in_=w1_grouped[:].rearrange("p t m j -> p (t m j)")
-        )
+        for u in range(2):
+            pair = slice(2 * P * u, 2 * P * (u + 1))
+            nc.vector.quantize_mx(
+                out=w1_codes[:, pair].bitcast(FP8X4),
+                scales=w1_scales[:, pair],
+                in_=w1_grouped[u][:].rearrange("p t m j -> p (t m j)"),
+            )
 
         neg_max = keep.tile([P, 1], F32, name="neg_max", tag="w2_grouped", align_bytes=MX_ALIGN)
         nc.vector.tensor_reduce(out=neg_max[:], in_=max_row[:, :P], axis=AXIS.X, op=ALU.max, negate=True)

@@ -107,7 +107,10 @@ def tile_picked_ygcb_relu_po_kernel(tc, x_words, x_scales, w1, w2, score, offs, 
         nc.sync.dma_start(out=score_table[ROW:, :], in_=score[0:1, :])
         w1_raw = keep.tile([P, PACK, H], F32, name="w1_raw", align_bytes=DMA_ALIGN)
         nc.sync.dma_start(out=w1_raw[:], in_=w1.rearrange("(p j) c -> p j c", j=PACK))
-        nc.sync.dma_start(out=scale_table[0:P:8, :].bitcast(I32), in_=x_scales[0].bitcast(I32))
+        for u in range(2):
+            nc.sync.dma_start(
+                out=scale_table[64 * u : 64 * u + 32 : PACK, :].bitcast(I32), in_=x_scales[0, 8 * u : 8 * u + 8, :].bitcast(I32)
+            )
         word_table = keep.tile([P, T], I32, name="word_table", align_bytes=DMA_ALIGN)
         nc.sync.dma_start(out=word_table[:], in_=x_words[0].rearrange("p c r -> p (c r)").bitcast(I32))
 
@@ -155,8 +158,11 @@ def tile_picked_ygcb_relu_po_kernel(tc, x_words, x_scales, w1, w2, score, offs, 
         cols = shared.tile([P, S // P], F32, name="cols", offset=PACK * P, align_bytes=MX_ALIGN)
         for h in range(HALVES):
             take_columns(cols, h)
-        for r in range(PACK):
-            nc.sync.dma_start(out=x_scale[r:P:32, :].bitcast(I32), in_=picked_scale[8 * r : P : 32, :].bitcast(I32))
+        for q in range(QUADS):
+            first = 64 * (q // 2) + 16 * (q % 2)
+            nc.sync.dma_start(
+                out=x_scale[32 * q : 32 * q + PACK, :].bitcast(I32), in_=picked_scale[first : first + 16 : PACK, :].bitcast(I32)
+            )
         w2_raw.append(load_w2_half(1, "scales_then_w2"))
 
         w1_codes = keep.tile([P, PACK * P], U32, name="w1_codes", align_bytes=MX_ALIGN)

@@ -107,10 +107,7 @@ def tile_picked_ygcb_relu_po_kernel(tc, x_words, x_scales, w1, w2, score, offs, 
         nc.sync.dma_start(out=score_table[ROW:, :], in_=score[0:1, :])
         w1_raw = keep.tile([P, PACK, H], F32, name="w1_raw", align_bytes=DMA_ALIGN)
         nc.sync.dma_start(out=w1_raw[:], in_=w1.rearrange("(p j) c -> p j c", j=PACK))
-        for u in range(2):
-            nc.sync.dma_start(
-                out=scale_table[64 * u : 64 * u + 32 : PACK, :].bitcast(I32), in_=x_scales[0, 8 * u : 8 * u + 8, :].bitcast(I32)
-            )
+        nc.sync.dma_start(out=scale_table[0:64:PACK, :].bitcast(I32), in_=x_scales[0].bitcast(I32))
         word_table = keep.tile([P, T], I32, name="word_table", align_bytes=DMA_ALIGN)
         nc.sync.dma_start(out=word_table[:], in_=x_words[0].rearrange("p c r -> p (c r)").bitcast(I32))
 
@@ -159,7 +156,7 @@ def tile_picked_ygcb_relu_po_kernel(tc, x_words, x_scales, w1, w2, score, offs, 
         for h in range(HALVES):
             take_columns(cols, h)
         for q in range(QUADS):
-            first = 64 * (q // 2) + 16 * (q % 2)
+            first = 16 * q
             nc.sync.dma_start(
                 out=x_scale[32 * q : 32 * q + PACK, :].bitcast(I32), in_=picked_scale[first : first + 16 : PACK, :].bitcast(I32)
             )

@@ -33,11 +33,11 @@ MAX_BANK = 3
 VECTOR_END = 2383
 SCALAR_END = 2896
 
-WIDTHS = (64, 64, 128, 256, 128, 256, 128)
+WIDTHS = (128, 128, 256, 128, 256, 128)
 STARTS = tuple(sum(WIDTHS[:c]) for c in range(len(WIDTHS)))
 CHUNKS = len(WIDTHS)
-CHUNK_BANKS = ((0,), (1,), (2,), (3, 4), (5,), (0, 6), (7,))
-OWN_END = STARTS[2]
+CHUNK_BANKS = ((0, 1), (2,), (3, 4), (5,), (0, 6), (7,))
+OWN_END = STARTS[1]
 
 OUT_WIDTHS = (256, 256, 128, 256, 128)
 OUT_STARTS = tuple(sum(OUT_WIDTHS[:c]) for c in range(len(OUT_WIDTHS)))
@@ -208,51 +208,62 @@ def tile_picked_ygcb_relu_po_kernel(tc, x_words, x_scales, w1, w2, score, offs, 
             keep.tile([P, PACK, BANK], BF16, name="z_planes0", tag="scales_then_w2", align_bytes=DMA_ALIGN),
             keep.tile([P, PACK, BANK], BF16, name="z_planes1", align_bytes=MX_ALIGN),
         ]
-        floor = z_planes[1][:, LAST, 0:2].bitcast(F32)
-        nc.gpsimd.memset(floor, 0.0)
         parts = [keep.tile([P, HALVES], F32, name="part%d" % t) for t in range(PACK)]
 
-        def weighted_sum(t, h):
+        def weighted_sum(t, h, factor):
             weighted = keep.tile([P, BANK], BF16, name="weighted%d_%d" % (t, h), tag="weighted%d_%d" % (t, h))
             nc.vector.scalar_tensor_tensor(
                 out=weighted[:],
                 in0=y[t, h][:],
-                scalar=1.0,
+                scalar=factor,
                 in1=weights[:, half(h)],
                 op0=ALU.mult,
                 op1=ALU.mult,
                 accum_out=parts[t][:, h : h + 1],
             )
 
-        def add_context(t):
-            context = keep.tile([P, 1], F32, name="context%d" % t)
-            engine = nc.vector if t == LAST else nc.gpsimd
-            engine.tensor_scalar(
-                out=context[:], in0=parts[t][:, 0:1], scalar1=parts[t][:, 1:2], scalar2=inv_total[:], op0=ALU.add, op1=ALU.mult
-            )
-            cuts = (0, BANK, S)
+        contexts = {}
+
+        def join(t):
+            contexts[t] = keep.tile([P, 1], F32, name="context%d" % t)
             if t == LAST:
-                nc.vector.tensor_scalar(
-                    out=z_planes[0][:, t, :OWN_END], in0=y[t, 0][:, :OWN_END], scalar1=context[:], scalar2=floor, op0=ALU.add, op1=ALU.max
-                )
-                cuts = tuple(c0 for c0 in STARTS if OWN_END <= c0 <= BANK) + (S,)
-            for c0, c1 in zip(cuts, cuts[1:]):
-                h = c0 // BANK
-                nc.scalar.activation(
-                    out=z_planes[h][:, t, c0 - BANK * h : c1 - BANK * h],
-                    in_=y[t, h][:, c0 - BANK * h : c1 - BANK * h],
-                    func=ACT.Relu,
-                    bias=context[:],
-                    scale=1.0,
+                nc.gpsimd.tensor_tensor(out=contexts[t][:], in0=parts[t][:, 0:1], in1=parts[t][:, 1:2], op=ALU.add)
+            else:
+                nc.gpsimd.tensor_scalar(
+                    out=contexts[t][:], in0=parts[t][:, 0:1], scalar1=parts[t][:, 1:2], scalar2=inv_total[:], op0=ALU.add, op1=ALU.mult
                 )
 
-        weighted_sum(*order[0])
+        def relu(t, c0, c1):
+            h = c0 // BANK
+            cols = slice(c0 - BANK * h, c1 - BANK * h)
+            nc.scalar.activation(out=z_planes[h][:, t, cols], in_=y[t, h][:, cols], func=ACT.Relu, bias=contexts[t][:], scale=1.0)
+
+        weighted_sum(0, 0, 1.0)
         inv_total = keep.tile([P, 1], F32, name="inv_total", tag="weighted0_0")
         nc.vector.reciprocal(inv_total[:], total[:])
-        for t, h in order[1:]:
-            weighted_sum(t, h)
+        for t, h in order[1 : HALVES * LAST]:
+            weighted_sum(t, h, 1.0)
             if h == HALVES - 1:
-                add_context(t)
+                join(t)
+                if t < LAST - 1:
+                    relu(t, 0, BANK)
+                    relu(t, BANK, S)
+        weighted_sum(LAST, 0, inv_total[:])
+        biased = keep.tile([P, OWN_END], F32, name="biased")
+        relu(LAST - 1, 0, OWN_END)
+        nc.scalar.activation(out=biased[:], in_=y[LAST, 0][:, :OWN_END], func=ACT.Identity, bias=parts[LAST][:, 0:1], scale=1.0)
+        relu(LAST - 1, OWN_END, BANK)
+        weighted_sum(LAST, 1, inv_total[:])
+        first_grouped = keep.tile([P, OWN_END, PACK], BF16, name="first_grouped", align_bytes=MX_ALIGN)
+        interleave(nc.vector.tensor_copy, first_grouped[:, :, :LAST], z_planes[0][:, :LAST, :OWN_END])
+        nc.vector.tensor_scalar(
+            out=first_grouped[:, :, LAST], in0=biased[:], scalar1=parts[LAST][:, 1:2], scalar2=0.0, op0=ALU.add, op1=ALU.max
+        )
+        join(LAST)
+        relu(LAST, STARTS[1], STARTS[2])
+        relu(LAST, STARTS[2], BANK)
+        relu(LAST - 1, BANK, S)
+        relu(LAST, BANK, S)
 
         out_rows = out_0.rearrange("(p t) j -> p t j", t=PACK)
         out_words = out_1[0].rearrange("p c r -> p (c r)").bitcast(I32)
@@ -315,7 +326,7 @@ def tile_picked_ygcb_relu_po_kernel(tc, x_words, x_scales, w1, w2, score, offs, 
                     in_=out_grouped[c][:, c0 : c0 + step, :].rearrange("p c t -> p (c t)"),
                 )
 
-        group_z(0)
+        z_grouped[0] = first_grouped
         for t in range(PACK):
             quantize_w2(t)
         second_product(0)

@@ -33,10 +33,10 @@ MAX_BANK = 3
 VECTOR_END = 2383
 SCALAR_END = 2896
 
-WIDTHS = (128, 128, 256, 128, 256, 128)
+WIDTHS = (128, 128, 128, 128, 256, 128, 128)
 STARTS = tuple(sum(WIDTHS[:c]) for c in range(len(WIDTHS)))
 CHUNKS = len(WIDTHS)
-CHUNK_BANKS = ((0, 1), (2,), (3, 4), (5,), (0, 6), (7,))
+CHUNK_BANKS = ((0, 1), (2,), (3,), (4,), (5, 6), (0,), (7,))
 OWN_END = STARTS[1]
 
 OUT_WIDTHS = (256, 256, 128, 256, 128)
@@ -211,7 +211,7 @@ def tile_picked_ygcb_relu_po_kernel(tc, x_words, x_scales, w1, w2, score, offs, 
         parts = [keep.tile([P, HALVES], F32, name="part%d" % t) for t in range(PACK)]
 
         def weighted_sum(t, h, factor):
-            weighted = keep.tile([P, BANK], BF16, name="weighted%d_%d" % (t, h), tag="weighted%d_%d" % (t, h))
+            weighted = keep.tile([P, BANK], BF16, name="weighted%d_%d" % (t, h), tag="weighted%d_%d" % (t, h), align_bytes=MX_ALIGN)
             nc.vector.scalar_tensor_tensor(
                 out=weighted[:],
                 in0=y[t, h][:],
@@ -227,7 +227,7 @@ def tile_picked_ygcb_relu_po_kernel(tc, x_words, x_scales, w1, w2, score, offs, 
         def join(t):
             contexts[t] = keep.tile([P, 1], F32, name="context%d" % t)
             if t == LAST:
-                nc.gpsimd.tensor_tensor(out=contexts[t][:], in0=parts[t][:, 0:1], in1=parts[t][:, 1:2], op=ALU.add)
+                nc.vector.tensor_tensor(out=contexts[t][:], in0=parts[t][:, 0:1], in1=parts[t][:, 1:2], op=ALU.add)
             else:
                 nc.gpsimd.tensor_scalar(
                     out=contexts[t][:], in0=parts[t][:, 0:1], scalar1=parts[t][:, 1:2], scalar2=inv_total[:], op0=ALU.add, op1=ALU.mult
@@ -239,7 +239,7 @@ def tile_picked_ygcb_relu_po_kernel(tc, x_words, x_scales, w1, w2, score, offs, 
             nc.scalar.activation(out=z_planes[h][:, t, cols], in_=y[t, h][:, cols], func=ACT.Relu, bias=contexts[t][:], scale=1.0)
 
         weighted_sum(0, 0, 1.0)
-        inv_total = keep.tile([P, 1], F32, name="inv_total", tag="weighted0_0")
+        inv_total = keep.tile([P, 1], F32, name="inv_total", tag="weighted0_0", align_bytes=MX_ALIGN)
         nc.vector.reciprocal(inv_total[:], total[:])
         for t, h in order[1 : HALVES * LAST]:
             weighted_sum(t, h, 1.0)
@@ -256,10 +256,10 @@ def tile_picked_ygcb_relu_po_kernel(tc, x_words, x_scales, w1, w2, score, offs, 
         weighted_sum(LAST, 1, inv_total[:])
         first_grouped = keep.tile([P, OWN_END, PACK], BF16, name="first_grouped", align_bytes=MX_ALIGN)
         interleave(nc.vector.tensor_copy, first_grouped[:, :, :LAST], z_planes[0][:, :LAST, :OWN_END])
+        join(LAST)
         nc.vector.tensor_scalar(
             out=first_grouped[:, :, LAST], in0=biased[:], scalar1=parts[LAST][:, 1:2], scalar2=0.0, op0=ALU.add, op1=ALU.max
         )
-        join(LAST)
         relu(LAST, STARTS[1], STARTS[2])
         relu(LAST, STARTS[2], BANK)
         relu(LAST - 1, BANK, S)
@@ -270,7 +270,7 @@ def tile_picked_ygcb_relu_po_kernel(tc, x_words, x_scales, w1, w2, score, offs, 
         out_codes = keep.tile([P, S], I32, name="out_codes", align_bytes=DMA_ALIGN)
         out_scales = keep.tile([P, STRIP], U8, name="out_scales", align_bytes=DMA_ALIGN)
         result = keep.tile([P, PACK, S], F32, name="result", align_bytes=DMA_ALIGN)
-        w2_codes = keep.tile([P, PACK * P], U32, name="w2_codes", align_bytes=MX_ALIGN)
+        w2_codes = keep.tile([P, PACK * P], U32, name="w2_codes", tag="weighted3_1", align_bytes=MX_ALIGN)
         w2_scales = keep.tile([P, PACK * P], U8, name="w2_scales", align_bytes=MX_ALIGN)
         z_grouped, out_grouped = {}, {}
 

@@ -33,10 +33,12 @@ MAX_BANK = 3
 VECTOR_END = 2383
 SCALAR_END = 2896
 
-WIDTHS = (128, 128, 128, 128, 256, 128, 128)
+GPSIMD_FROM = 96
+
+WIDTHS = (128,) * 8
 STARTS = tuple(sum(WIDTHS[:c]) for c in range(len(WIDTHS)))
 CHUNKS = len(WIDTHS)
-CHUNK_BANKS = ((0, 1), (2,), (3,), (4,), (5, 6), (0,), (7,))
+CHUNK_BANKS = ((0, 1), (2,), (3,), (4,), (5,), (6,), (0,), (7,))
 OWN_END = STARTS[1]
 
 OUT_WIDTHS = (256, 256, 128, 256, 128)
@@ -108,7 +110,7 @@ def tile_picked_ygcb_relu_po_kernel(tc, x_words, x_scales, w1, w2, score, offs, 
         w1_raw = keep.tile([P, PACK, H], F32, name="w1_raw", align_bytes=DMA_ALIGN)
         nc.sync.dma_start(out=w1_raw[:], in_=w1.rearrange("(p j) c -> p j c", j=PACK))
         nc.sync.dma_start(out=scale_table[0:64:PACK, :].bitcast(I32), in_=x_scales[0].bitcast(I32))
-        word_table = keep.tile([P, T], I32, name="word_table", align_bytes=DMA_ALIGN)
+        word_table = keep.tile([P, T], I32, name="word_table", tag="words_then_zero", align_bytes=DMA_ALIGN)
         nc.sync.dma_start(out=word_table[:], in_=x_words[0].rearrange("p c r -> p (c r)").bitcast(I32))
 
         def load_w2_half(u, tag):
@@ -201,8 +203,18 @@ def tile_picked_ygcb_relu_po_kernel(tc, x_words, x_scales, w1, w2, score, offs, 
             product(y[t, h][:], w1_codes, w1_scales, t, x_codes[:, half(h)], x_scale[:, half(h)])
 
         w2_grouped = keep.tile([P, PACK, P, PACK], BF16, name="w2_grouped", tag="w2_grouped", align_bytes=MX_ALIGN)
-        for u in range(2):
-            deal_columns(nc, w2_grouped[:, :, u * (P // 2) : (u + 1) * (P // 2), :], w2_raw[u][:])
+        deal_columns(nc, w2_grouped[:, :, : P // 2, :], w2_raw[0][:])
+        deal_columns(nc, w2_grouped[:, :, P // 2 : GPSIMD_FROM, :], w2_raw[1][:, :, : PACK * (GPSIMD_FROM - P // 2)])
+        late_zero = keep.tile([P, 1], F32, name="late_zero", tag="words_then_zero", align_bytes=DMA_ALIGN)
+        nc.gpsimd.memset(late_zero[:], 0.0)
+        nc.gpsimd.tensor_scalar(
+            out=w2_grouped[:, :, GPSIMD_FROM:, :].rearrange("p t m j -> p m t j"),
+            in0=w2_raw[1][:].rearrange("p j (m t) -> p m t j", t=PACK)[:, GPSIMD_FROM - P // 2 :],
+            scalar1=1.0,
+            scalar2=late_zero[:],
+            op0=ALU.mult,
+            op1=ALU.add,
+        )
 
         z_planes = [
             keep.tile([P, PACK, BANK], BF16, name="z_planes0", tag="scales_then_w2", align_bytes=DMA_ALIGN),

@@ -33,12 +33,12 @@ MAX_BANK = 3
 VECTOR_END = 2383
 SCALAR_END = 2896
 
-GPSIMD_FROM = 96
+QUARTER = 768
 
-WIDTHS = (128,) * 8
+WIDTHS = (128, 128, 128, 128, 256, 128, 128)
 STARTS = tuple(sum(WIDTHS[:c]) for c in range(len(WIDTHS)))
 CHUNKS = len(WIDTHS)
-CHUNK_BANKS = ((0, 1), (2,), (3,), (4,), (5,), (6,), (0,), (7,))
+CHUNK_BANKS = ((0, 1), (2,), (3,), (4,), (5, 6), (0,), (7,))
 OWN_END = STARTS[1]
 
 OUT_WIDTHS = (256, 256, 128, 256, 128)
@@ -110,7 +110,7 @@ def tile_picked_ygcb_relu_po_kernel(tc, x_words, x_scales, w1, w2, score, offs, 
         w1_raw = keep.tile([P, PACK, H], F32, name="w1_raw", align_bytes=DMA_ALIGN)
         nc.sync.dma_start(out=w1_raw[:], in_=w1.rearrange("(p j) c -> p j c", j=PACK))
         nc.sync.dma_start(out=scale_table[0:64:PACK, :].bitcast(I32), in_=x_scales[0].bitcast(I32))
-        word_table = keep.tile([P, T], I32, name="word_table", tag="words_then_zero", align_bytes=DMA_ALIGN)
+        word_table = keep.tile([P, T], I32, name="word_table", align_bytes=DMA_ALIGN)
         nc.sync.dma_start(out=word_table[:], in_=x_words[0].rearrange("p c r -> p (c r)").bitcast(I32))
 
         def load_w2_half(u, tag):
@@ -150,13 +150,13 @@ def tile_picked_ygcb_relu_po_kernel(tc, x_words, x_scales, w1, w2, score, offs, 
 
         cast_w1(0, nc.vector.tensor_copy, "w1_first_planes")
         cast_w1(1, nc.scalar.copy, "picked_then_w1")
-        col_max = keep.tile([P, 1], F32, name="col_max", tag="max_then_codes", align_bytes=MX_ALIGN)
-        nc.vector.tensor_reduce(out=col_max[:], in_=max_cols[:, : S // P], axis=AXIS.X, op=ALU.max)
+        col_max = keep.tile([P, 1], F32, name="col_max")
+        cols = keep.tile([P, S // P], F32, name="cols")
+        nc.vector.tensor_scalar(
+            out=cols[:], in0=max_cols[:, : S // P], scalar1=1.0, scalar2=None, op0=ALU.mult, op1=ALU.max, accum_out=col_max[:]
+        )
         max_row = bank(MAX_BANK)
         nc.tensor.transpose(max_row[:, :P], col_max[:].to_broadcast([P, P]), ident[:])
-        cols = shared.tile([P, S // P], F32, name="cols", offset=PACK * P, align_bytes=MX_ALIGN)
-        for h in range(HALVES):
-            take_columns(cols, h)
         for q in range(QUADS):
             first = 16 * q
             nc.sync.dma_start(
@@ -175,7 +175,10 @@ def tile_picked_ygcb_relu_po_kernel(tc, x_words, x_scales, w1, w2, score, offs, 
             )
 
         neg_max = keep.tile([P, 1], F32, name="neg_max", tag="w2_grouped", align_bytes=MX_ALIGN)
-        nc.vector.tensor_reduce(out=neg_max[:], in_=max_row[:, :P], axis=AXIS.X, op=ALU.max, negate=True)
+        negated = keep.tile([P, P], F32, name="negated", tag="max_then_codes", align_bytes=MX_ALIGN)
+        nc.vector.tensor_scalar(
+            out=negated[:], in0=max_row[:, :P], scalar1=-1.0, scalar2=None, op0=ALU.mult, op1=ALU.min, accum_out=neg_max[:]
+        )
         spread = []
         for h in range(HALVES):
             spread.append(bank(HALVES * (LAST - 1) + h))
@@ -198,91 +201,99 @@ def tile_picked_ygcb_relu_po_kernel(tc, x_words, x_scales, w1, w2, score, offs, 
 
         y = {}
         order = [(t, h) for t in range(PACK) for h in range(HALVES)]
-        for t, h in [(t, h) for h in range(HALVES) for t in range(2)] + order[2 * HALVES :]:
-            y[t, h] = bank(HALVES * t + h)
-            product(y[t, h][:], w1_codes, w1_scales, t, x_codes[:, half(h)], x_scale[:, half(h)])
+
+        def first_product(t, c0, c1, b):
+            y[t, c0] = bank(b)
+            product(y[t, c0][:, : c1 - c0], w1_codes, w1_scales, t, x_codes[:, c0:c1], x_scale[:, c0:c1])
+
+        first_product(0, 0, BANK, 0)
+        first_product(0, BANK, QUARTER, 1)
+        first_product(0, QUARTER, S, 7)
+        for t, h in order[HALVES:-1]:
+            first_product(t, BANK * h, BANK * (h + 1), HALVES * t + h)
 
         w2_grouped = keep.tile([P, PACK, P, PACK], BF16, name="w2_grouped", tag="w2_grouped", align_bytes=MX_ALIGN)
-        deal_columns(nc, w2_grouped[:, :, : P // 2, :], w2_raw[0][:])
-        deal_columns(nc, w2_grouped[:, :, P // 2 : GPSIMD_FROM, :], w2_raw[1][:, :, : PACK * (GPSIMD_FROM - P // 2)])
-        late_zero = keep.tile([P, 1], F32, name="late_zero", tag="words_then_zero", align_bytes=DMA_ALIGN)
-        nc.gpsimd.memset(late_zero[:], 0.0)
-        nc.gpsimd.tensor_scalar(
-            out=w2_grouped[:, :, GPSIMD_FROM:, :].rearrange("p t m j -> p m t j"),
-            in0=w2_raw[1][:].rearrange("p j (m t) -> p m t j", t=PACK)[:, GPSIMD_FROM - P // 2 :],
-            scalar1=1.0,
-            scalar2=late_zero[:],
-            op0=ALU.mult,
-            op1=ALU.add,
-        )
+        for u in range(2):
+            deal_columns(nc, w2_grouped[:, :, u * (P // 2) : (u + 1) * (P // 2), :], w2_raw[u][:])
 
         z_planes = [
             keep.tile([P, PACK, BANK], BF16, name="z_planes0", tag="scales_then_w2", align_bytes=DMA_ALIGN),
             keep.tile([P, PACK, BANK], BF16, name="z_planes1", align_bytes=MX_ALIGN),
         ]
-        parts = [keep.tile([P, HALVES], F32, name="part%d" % t) for t in range(PACK)]
+        parts = {}
 
-        def weighted_sum(t, h, factor):
-            weighted = keep.tile([P, BANK], BF16, name="weighted%d_%d" % (t, h), tag="weighted%d_%d" % (t, h), align_bytes=MX_ALIGN)
+        def weighted_sum(t, c0, c1, factor):
+            weighted = keep.tile([P, c1 - c0], BF16, name="weighted%d_%d" % (t, c0), tag="weighted%d_%d" % (t, c0), align_bytes=MX_ALIGN)
+            parts[t, c0] = keep.tile([P, 1], F32, name="part%d_%d" % (t, c0))
             nc.vector.scalar_tensor_tensor(
                 out=weighted[:],
-                in0=y[t, h][:],
+                in0=y[t, c0][:, : c1 - c0],
                 scalar=factor,
-                in1=weights[:, half(h)],
+                in1=weights[:, c0:c1],
                 op0=ALU.mult,
                 op1=ALU.mult,
-                accum_out=parts[t][:, h : h + 1],
+                accum_out=parts[t, c0][:],
             )
 
         contexts = {}
 
-        def join(t):
+        def join(t, first, second):
             contexts[t] = keep.tile([P, 1], F32, name="context%d" % t)
-            if t == LAST:
-                nc.vector.tensor_tensor(out=contexts[t][:], in0=parts[t][:, 0:1], in1=parts[t][:, 1:2], op=ALU.add)
-            else:
-                nc.gpsimd.tensor_scalar(
-                    out=contexts[t][:], in0=parts[t][:, 0:1], scalar1=parts[t][:, 1:2], scalar2=inv_total[:], op0=ALU.add, op1=ALU.mult
-                )
+            nc.gpsimd.tensor_scalar(out=contexts[t][:], in0=first[:], scalar1=second[:], scalar2=inv_total[:], op0=ALU.add, op1=ALU.mult)
 
-        def relu(t, c0, c1):
+        def relu(t, start, c0, c1):
             h = c0 // BANK
-            cols = slice(c0 - BANK * h, c1 - BANK * h)
-            nc.scalar.activation(out=z_planes[h][:, t, cols], in_=y[t, h][:, cols], func=ACT.Relu, bias=contexts[t][:], scale=1.0)
+            nc.scalar.activation(
+                out=z_planes[h][:, t, c0 - BANK * h : c1 - BANK * h],
+                in_=y[t, start][:, c0 - start : c1 - start],
+                func=ACT.Relu,
+                bias=contexts[t][:],
+                scale=1.0,
+            )
 
-        weighted_sum(0, 0, 1.0)
+        weighted_sum(0, 0, BANK, 1.0)
         inv_total = keep.tile([P, 1], F32, name="inv_total", tag="weighted0_0", align_bytes=MX_ALIGN)
         nc.vector.reciprocal(inv_total[:], total[:])
-        for t, h in order[1 : HALVES * LAST]:
-            weighted_sum(t, h, 1.0)
-            if h == HALVES - 1:
-                join(t)
-                if t < LAST - 1:
-                    relu(t, 0, BANK)
-                    relu(t, BANK, S)
-        weighted_sum(LAST, 0, inv_total[:])
+        weighted_sum(0, BANK, QUARTER, 1.0)
+        three_quarters = keep.tile([P, 1], F32, name="three_quarters")
+        nc.gpsimd.tensor_tensor(out=three_quarters[:], in0=parts[0, 0][:], in1=parts[0, BANK][:], op=ALU.add)
+        weighted_sum(0, QUARTER, S, 1.0)
+        join(0, three_quarters, parts[0, QUARTER])
+        relu(0, QUARTER, QUARTER, S)
+        relu(0, 0, 0, BANK)
+        relu(0, BANK, BANK, QUARTER)
+        first_product(LAST, BANK, S, 7)
+        for t in (1, 2):
+            weighted_sum(t, 0, BANK, 1.0)
+            weighted_sum(t, BANK, S, 1.0)
+            join(t, parts[t, 0], parts[t, BANK])
+            if t == 1:
+                relu(t, 0, 0, BANK)
+                relu(t, BANK, BANK, S)
+        weighted_sum(LAST, 0, BANK, inv_total[:])
         biased = keep.tile([P, OWN_END], F32, name="biased")
-        relu(LAST - 1, 0, OWN_END)
-        nc.scalar.activation(out=biased[:], in_=y[LAST, 0][:, :OWN_END], func=ACT.Identity, bias=parts[LAST][:, 0:1], scale=1.0)
-        relu(LAST - 1, OWN_END, BANK)
-        weighted_sum(LAST, 1, inv_total[:])
+        relu(LAST - 1, 0, 0, OWN_END)
+        nc.scalar.activation(out=biased[:], in_=y[LAST, 0][:, :OWN_END], func=ACT.Identity, bias=parts[LAST, 0][:], scale=1.0)
+        relu(LAST - 1, 0, OWN_END, BANK)
+        weighted_sum(LAST, BANK, S, inv_total[:])
         first_grouped = keep.tile([P, OWN_END, PACK], BF16, name="first_grouped", align_bytes=MX_ALIGN)
         interleave(nc.vector.tensor_copy, first_grouped[:, :, :LAST], z_planes[0][:, :LAST, :OWN_END])
-        join(LAST)
+        contexts[LAST] = keep.tile([P, 1], F32, name="last_context")
+        nc.vector.tensor_tensor(out=contexts[LAST][:], in0=parts[LAST, 0][:], in1=parts[LAST, BANK][:], op=ALU.add)
         nc.vector.tensor_scalar(
-            out=first_grouped[:, :, LAST], in0=biased[:], scalar1=parts[LAST][:, 1:2], scalar2=0.0, op0=ALU.add, op1=ALU.max
+            out=first_grouped[:, :, LAST], in0=biased[:], scalar1=parts[LAST, BANK][:], scalar2=0.0, op0=ALU.add, op1=ALU.max
         )
-        relu(LAST, STARTS[1], STARTS[2])
-        relu(LAST, STARTS[2], BANK)
-        relu(LAST - 1, BANK, S)
-        relu(LAST, BANK, S)
+        relu(LAST, 0, STARTS[1], STARTS[2])
+        relu(LAST, 0, STARTS[2], BANK)
+        relu(LAST - 1, BANK, BANK, S)
+        relu(LAST, BANK, BANK, S)
 
         out_rows = out_0.rearrange("(p t) j -> p t j", t=PACK)
         out_words = out_1[0].rearrange("p c r -> p (c r)").bitcast(I32)
         out_codes = keep.tile([P, S], I32, name="out_codes", align_bytes=DMA_ALIGN)
         out_scales = keep.tile([P, STRIP], U8, name="out_scales", align_bytes=DMA_ALIGN)
         result = keep.tile([P, PACK, S], F32, name="result", align_bytes=DMA_ALIGN)
-        w2_codes = keep.tile([P, PACK * P], U32, name="w2_codes", tag="weighted3_1", align_bytes=MX_ALIGN)
+        w2_codes = keep.tile([P, PACK * P], U32, name="w2_codes", tag="weighted3_512", align_bytes=MX_ALIGN)
         w2_scales = keep.tile([P, PACK * P], U8, name="w2_scales", align_bytes=MX_ALIGN)
         z_grouped, out_grouped = {}, {}
 

@@ -223,7 +223,7 @@ def tile_picked_ygcb_relu_po_kernel(tc, x_words, x_scales, w1, w2, score, offs, 
         parts = {}
 
         def weighted_sum(t, c0, c1, factor):
-            weighted = keep.tile([P, c1 - c0], BF16, name="weighted%d_%d" % (t, c0), tag="weighted%d_%d" % (t, c0), align_bytes=MX_ALIGN)
+            weighted = keep.tile([P, c1 - c0], BF16, name="weighted%d_%d" % (t, c0), tag="weighted%d_%d" % ((0, BANK) if (t, c0) == (1, 0) else (t, c0)), align_bytes=MX_ALIGN)
             parts[t, c0] = keep.tile([P, 1], F32, name="part%d_%d" % (t, c0))
             nc.vector.scalar_tensor_tensor(
                 out=weighted[:],

from contextlib import ExitStack

import concourse.mybir as mybir
from concourse.masks import make_identity

K, T, S, H, N = 512, 4096, 1024, 512, 512
FLOPS = 2 * K * H * S + 2 * H * N * S

F32 = mybir.dt.float32
BF16 = mybir.dt.bfloat16
I32 = mybir.dt.int32
U32 = mybir.dt.uint32
U16 = mybir.dt.uint16
U8 = mybir.dt.uint8
FP8X4 = mybir.dt.float8_e4m3fn_x4
ALU = mybir.AluOpType
ACT = mybir.ActivationFunctionType
AXIS = mybir.AxisListType

P = 128
PACK = 4
BANK = 512
HALVES = S // BANK
BLOCKS = BANK // P
QUADS = 4
LAST = PACK - 1
MX_ALIGN = 64
DMA_ALIGN = 256
RUN = 4
ROW = P - 1
MAX_BANK = 3

VECTOR_END = 2383
SCALAR_END = 2896

QUARTER = 768

WIDTHS = (128, 128, 128, 128, 256, 128, 128)
STARTS = tuple(sum(WIDTHS[:c]) for c in range(len(WIDTHS)))
CHUNKS = len(WIDTHS)
CHUNK_BANKS = ((0, 1), (2,), (3,), (4,), (5, 6), (0,), (7,))
OWN_END = STARTS[1]

OUT_WIDTHS = (256, 256, 128, 256, 128)
OUT_STARTS = tuple(sum(OUT_WIDTHS[:c]) for c in range(len(OUT_WIDTHS)))
PIECES = len(OUT_WIDTHS)
STRIP = S // QUADS


def interleave(engine_copy, out, planes):
    engine_copy(
        out=out.rearrange("p (c i) t -> p c t i", i=RUN),
        in_=planes.rearrange("p t (c i) -> p c t i", i=RUN),
    )


def deal_columns(nc, out, raw):
    nc.scalar.copy(out=out.rearrange("p t m j -> p m j t"), in_=raw.rearrange("p j (m t) -> p m j t", t=PACK))


def tile_picked_ygcb_relu_po_kernel(tc, x_words, x_scales, w1, w2, score, offs, out_0, out_1, out_2):
    nc = tc.nc
    with ExitStack() as ctx:
        keep = ctx.enter_context(tc.tile_pool(name="keep", bufs=1))
        shared = ctx.enter_context(tc.tile_pool(name="shared", bufs=1))
        psum = ctx.enter_context(tc.psum_pool(name="psum", bufs=1))

        def bank(b):
            return psum.tile([P, BANK], F32, name="bank%d" % b)

        def half(h):
            return slice(BANK * h, BANK * (h + 1))

        def plane_cols(t):
            return slice(P * t, P * (t + 1))

        def product(out, w_codes, w_scales, t, codes, scales):
            nc.tensor.matmul_mx(
                out=out,
                lhsT=w_codes[:, plane_cols(t)].bitcast(FP8X4),
                lhsT_scale=w_scales[:, plane_cols(t)],
                rhs=codes.bitcast(FP8X4),
                rhs_scale=scales,
                start=True,
                stop=True,
            )

        offsets = keep.tile([P, S // 16], U16, name="offsets")
        nc.sync.dma_start(offsets[:], offs)

        def half_list(h):
            return offsets[:, h * (BANK // 16) : (h + 1) * (BANK // 16)]

        scale_table = keep.tile([P, T], U8, name="scale_table", tag="scales_then_w2", align_bytes=DMA_ALIGN)
        zero = keep.tile([P, 1], F32, name="zero")
        nc.gpsimd.memset(zero[:], 0.0)
        nc.gpsimd.memset(scale_table[:].bitcast(I32), 0)
        score_table = keep.tile([P, T], F32, name="score_table", align_bytes=DMA_ALIGN)
        nc.vector.memset(score_table[:ROW, :VECTOR_END].bitcast(I32), 0)
        nc.scalar.copy(
            out=score_table[:ROW, VECTOR_END:SCALAR_END], in_=zero[:ROW, :].to_broadcast([ROW, SCALAR_END - VECTOR_END])
        )
        nc.gpsimd.memset(score_table[:ROW, SCALAR_END:].bitcast(I32), 0)
        ident = keep.tile([P, P], F32, name="ident")
        make_identity(nc, ident[:])
        x_scale = keep.tile([P, S], U8, name="x_scale", align_bytes=DMA_ALIGN)
        nc.gpsimd.memset(x_scale[:].bitcast(I32), 0)

        nc.sync.dma_start(out=score_table[ROW:, :], in_=score[0:1, :])
        w1_raw = keep.tile([P, PACK, H], F32, name="w1_raw", align_bytes=DMA_ALIGN)
        nc.sync.dma_start(out=w1_raw[:], in_=w1.rearrange("(p j) c -> p j c", j=PACK))
        nc.sync.dma_start(out=scale_table[0:64:PACK, :].bitcast(I32), in_=x_scales[0].bitcast(I32))
        word_table = keep.tile([P, T], I32, name="word_table", align_bytes=DMA_ALIGN)
        nc.sync.dma_start(out=word_table[:], in_=x_words[0].rearrange("p c r -> p (c r)").bitcast(I32))

        def load_w2_half(u, tag):
            raw = keep.tile([P, PACK, N // 2], F32, name="w2_raw%d" % u, tag=tag, align_bytes=DMA_ALIGN)
            nc.sync.dma_start(out=raw[:], in_=w2.rearrange("(p j) c -> p j c", j=PACK)[:, :, u * (N // 2) : (u + 1) * (N // 2)])
            return raw

        w2_raw = [load_w2_half(0, "w2_first_half")]

        picked = keep.tile([P, S], F32, name="picked", tag="picked_then_w1", align_bytes=DMA_ALIGN)
        for h in range(HALVES):
            nc.scalar.activation(out=picked[:, half(h)], in_=score_table[:].indirect(half_list(h)), func=ACT.Copy)
        max_cols = shared.tile([P, 2 * P], F32, name="max_cols", offset=0, align_bytes=MX_ALIGN)
        turned = []

        def take_columns(out, h):
            nc.scalar.copy(
                out=out[:, BLOCKS * h : BLOCKS * (h + 1)], in_=turned[h][:].rearrange("p (c n) -> p c n", c=BLOCKS)[:, :, ROW]
            )

        for h in range(HALVES):
            turned.append(bank(HALVES * LAST + h))
            for c in range(BLOCKS):
                nc.tensor.transpose(turned[h][:, plane_cols(c)], picked[:, BANK * h + P * c : BANK * h + P * (c + 1)], ident[:])
            take_columns(max_cols, h)

        picked_scale = keep.tile([P, S], U8, name="picked_scale", align_bytes=DMA_ALIGN)
        nc.vector.tensor_copy(picked_scale[:], scale_table[:].indirect(offsets[:]))
        w1_grouped = []

        def cast_w1(u, copy, tag):
            w1_grouped.append(keep.tile([P, 2, P, PACK], BF16, name="w1_grouped%d" % u, tag=tag, align_bytes=DMA_ALIGN))
            copy(
                out=w1_grouped[u][:].rearrange("p t m j -> p m t j"),
                in_=w1_raw[:].rearrange("p j (m t) -> p m t j", t=PACK)[:, :, 2 * u : 2 * u + 2],
            )

        cast_w1(0, nc.vector.tensor_copy, "w1_first_planes")
        cast_w1(1, nc.scalar.copy, "picked_then_w1")
        col_max = keep.tile([P, 1], F32, name="col_max")
        cols = keep.tile([P, S // P], F32, name="cols")
        nc.vector.tensor_scalar(
            out=cols[:], in0=max_cols[:, : S // P], scalar1=1.0, scalar2=None, op0=ALU.mult, op1=ALU.max, accum_out=col_max[:]
        )
        max_row = bank(MAX_BANK)
        nc.tensor.transpose(max_row[:, :P], col_max[:].to_broadcast([P, P]), ident[:])
        for q in range(QUADS):
            first = 16 * q
            nc.sync.dma_start(
                out=x_scale[32 * q : 32 * q + PACK, :].bitcast(I32), in_=picked_scale[first : first + 16 : PACK, :].bitcast(I32)
            )
        w2_raw.append(load_w2_half(1, "scales_then_w2"))

        w1_codes = keep.tile([P, PACK * P], U32, name="w1_codes", align_bytes=MX_ALIGN)
        w1_scales = shared.tile([P, PACK * P], U8, name="w1_scales", offset=0, align_bytes=MX_ALIGN)
        for u in range(2):
            pair = slice(2 * P * u, 2 * P * (u + 1))
            nc.vector.quantize_mx(
                out=w1_codes[:, pair].bitcast(FP8X4),
                scales=w1_scales[:, pair],
                in_=w1_grouped[u][:].rearrange("p t m j -> p (t m j)"),
            )

        neg_max = keep.tile([P, 1], F32, name="neg_max", tag="w2_grouped", align_bytes=MX_ALIGN)
        negated = keep.tile([P, P], F32, name="negated", tag="max_then_codes", align_bytes=MX_ALIGN)
        nc.vector.tensor_scalar(
            out=negated[:], in0=max_row[:, :P], scalar1=-1.0, scalar2=None, op0=ALU.mult, op1=ALU.min, accum_out=neg_max[:]
        )
        spread = []
        for h in range(HALVES):
            spread.append(bank(HALVES * (LAST - 1) + h))
            for c in range(BLOCKS):
                column = cols[:, BLOCKS * h + c : BLOCKS * h + c + 1]
                nc.tensor.transpose(spread[h][:, plane_cols(c)], column.to_broadcast([P, P]), ident[:])
        weights = keep.tile([P, S], F32, name="weights")
        totals = keep.tile([P, HALVES], F32, name="totals")
        for h in range(HALVES):
            nc.scalar.activation(
                out=weights[:, half(h)], in_=spread[h][:], func=ACT.Exp, bias=neg_max[:], scale=1.0, accum_out=totals[:, h : h + 1]
            )

        x_codes = keep.tile([P, S], U32, name="x_codes", tag="max_then_codes", align_bytes=MX_ALIGN)
        for h in range(HALVES):
            nc.vector.tensor_copy(x_codes[:, half(h)], word_table[:].bitcast(U32).indirect(half_list(h)))

        total = keep.tile([P, 1], F32, name="total")
        nc.gpsimd.tensor_tensor(out=total[:], in0=totals[:, 0:1], in1=totals[:, 1:2], op=ALU.add)

        y = {}
        order = [(t, h) for t in range(PACK) for h in range(HALVES)]

        def first_product(t, c0, c1, b):
            y[t, c0] = bank(b)
            product(y[t, c0][:, : c1 - c0], w1_codes, w1_scales, t, x_codes[:, c0:c1], x_scale[:, c0:c1])

        first_product(0, 0, BANK, 0)
        first_product(0, BANK, QUARTER, 1)
        first_product(0, QUARTER, S, 7)
        for t, h in order[HALVES:-1]:
            first_product(t, BANK * h, BANK * (h + 1), HALVES * t + h)

        w2_grouped = keep.tile([P, PACK, P, PACK], BF16, name="w2_grouped", tag="w2_grouped", align_bytes=MX_ALIGN)
        for u in range(2):
            deal_columns(nc, w2_grouped[:, :, u * (P // 2) : (u + 1) * (P // 2), :], w2_raw[u][:])

        z_planes = [
            keep.tile([P, PACK, BANK], BF16, name="z_planes0", tag="scales_then_w2", align_bytes=DMA_ALIGN),
            keep.tile([P, PACK, BANK], BF16, name="z_planes1", align_bytes=MX_ALIGN),
        ]
        parts = {}

        def weighted_sum(t, c0, c1, factor):
            weighted = keep.tile([P, c1 - c0], BF16, name="weighted%d_%d" % (t, c0), tag="weighted%d_%d" % ((0, BANK) if (t, c0) == (1, 0) else (t, c0)), align_bytes=MX_ALIGN)
            parts[t, c0] = keep.tile([P, 1], F32, name="part%d_%d" % (t, c0))
            nc.vector.scalar_tensor_tensor(
                out=weighted[:],
                in0=y[t, c0][:, : c1 - c0],
                scalar=factor,
                in1=weights[:, c0:c1],
                op0=ALU.mult,
                op1=ALU.mult,
                accum_out=parts[t, c0][:],
            )

        contexts = {}

        def join(t, first, second):
            contexts[t] = keep.tile([P, 1], F32, name="context%d" % t)
            nc.gpsimd.tensor_scalar(out=contexts[t][:], in0=first[:], scalar1=second[:], scalar2=inv_total[:], op0=ALU.add, op1=ALU.mult)

        def relu(t, start, c0, c1):
            h = c0 // BANK
            nc.scalar.activation(
                out=z_planes[h][:, t, c0 - BANK * h : c1 - BANK * h],
                in_=y[t, start][:, c0 - start : c1 - start],
                func=ACT.Relu,
                bias=contexts[t][:],
                scale=1.0,
            )

        weighted_sum(0, 0, BANK, 1.0)
        inv_total = keep.tile([P, 1], F32, name="inv_total", tag="weighted0_0", align_bytes=MX_ALIGN)
        nc.vector.reciprocal(inv_total[:], total[:])
        weighted_sum(0, BANK, QUARTER, 1.0)
        three_quarters = keep.tile([P, 1], F32, name="three_quarters")
        nc.gpsimd.tensor_tensor(out=three_quarters[:], in0=parts[0, 0][:], in1=parts[0, BANK][:], op=ALU.add)
        weighted_sum(0, QUARTER, S, 1.0)
        join(0, three_quarters, parts[0, QUARTER])
        relu(0, QUARTER, QUARTER, S)
        relu(0, 0, 0, BANK)
        relu(0, BANK, BANK, QUARTER)
        first_product(LAST, BANK, S, 7)
        for t in (1, 2):
            weighted_sum(t, 0, BANK, 1.0)
            weighted_sum(t, BANK, S, 1.0)
            join(t, parts[t, 0], parts[t, BANK])
            if t == 1:
                relu(t, 0, 0, BANK)
                relu(t, BANK, BANK, S)
        weighted_sum(LAST, 0, BANK, inv_total[:])
        biased = keep.tile([P, OWN_END], F32, name="biased")
        relu(LAST - 1, 0, 0, OWN_END)
        nc.scalar.activation(out=biased[:], in_=y[LAST, 0][:, :OWN_END], func=ACT.Identity, bias=parts[LAST, 0][:], scale=1.0)
        relu(LAST - 1, 0, OWN_END, BANK)
        weighted_sum(LAST, BANK, S, inv_total[:])
        first_grouped = keep.tile([P, OWN_END, PACK], BF16, name="first_grouped", align_bytes=MX_ALIGN)
        interleave(nc.vector.tensor_copy, first_grouped[:, :, :LAST], z_planes[0][:, :LAST, :OWN_END])
        contexts[LAST] = keep.tile([P, 1], F32, name="last_context")
        nc.vector.tensor_tensor(out=contexts[LAST][:], in0=parts[LAST, 0][:], in1=parts[LAST, BANK][:], op=ALU.add)
        nc.vector.tensor_scalar(
            out=first_grouped[:, :, LAST], in0=biased[:], scalar1=parts[LAST, BANK][:], scalar2=0.0, op0=ALU.add, op1=ALU.max
        )
        relu(LAST, 0, STARTS[1], STARTS[2])
        relu(LAST, 0, STARTS[2], BANK)
        relu(LAST - 1, BANK, BANK, S)
        relu(LAST, BANK, BANK, S)

        out_rows = out_0.rearrange("(p t) j -> p t j", t=PACK)
        out_words = out_1[0].rearrange("p c r -> p (c r)").bitcast(I32)
        out_codes = keep.tile([P, S], I32, name="out_codes", align_bytes=DMA_ALIGN)
        out_scales = keep.tile([P, STRIP], U8, name="out_scales", align_bytes=DMA_ALIGN)
        result = keep.tile([P, PACK, S], F32, name="result", align_bytes=DMA_ALIGN)
        w2_codes = keep.tile([P, PACK * P], U32, name="w2_codes", tag="weighted3_512", align_bytes=MX_ALIGN)
        w2_scales = keep.tile([P, PACK * P], U8, name="w2_scales", align_bytes=MX_ALIGN)
        z_grouped, out_grouped = {}, {}

        def chunk(c):
            return slice(STARTS[c], STARTS[c] + WIDTHS[c])

        def quantize_w2(t):
            nc.vector.quantize_mx(
                out=w2_codes[:, plane_cols(t)].bitcast(FP8X4),
                scales=w2_scales[:, plane_cols(t)],
                in_=w2_grouped[:, t, :, :].rearrange("p m j -> p (m j)"),
            )

        def group_z(c):
            z_grouped[c] = keep.tile([P, WIDTHS[c], PACK], BF16, name="z_grouped%d" % c, align_bytes=MX_ALIGN)
            h, c0 = divmod(STARTS[c], BANK)
            interleave(nc.vector.tensor_copy, z_grouped[c][:], z_planes[h][:, :, c0 : c0 + WIDTHS[c]])

        def second_product(c):
            width = WIDTHS[c]
            z_codes = keep.tile([P, width], U32, name="z_codes%d" % c, align_bytes=MX_ALIGN)
            z_scales = keep.tile([P, width], U8, name="z_scales%d" % c, align_bytes=MX_ALIGN)
            nc.vector.quantize_mx(
                out=z_codes[:].bitcast(FP8X4), scales=z_scales[:], in_=z_grouped[c][:].rearrange("p c t -> p (c t)")
            )
            per_bank = PACK // len(CHUNK_BANKS[c])
            for n, b in enumerate(CHUNK_BANKS[c]):
                acc = bank(b)
                t0 = n * per_bank
                for v in range(per_bank):
                    product(acc[:, width * v : width * (v + 1)], w2_codes, w2_scales, t0 + v, z_codes[:], z_scales[:])
                nc.scalar.copy(
                    out=result[:, t0 : t0 + per_bank, chunk(c)],
                    in_=acc[:, : per_bank * width].rearrange("p (t c) -> p t c", t=per_bank),
                )
                nc.sync.dma_start(out=out_rows[:, t0 : t0 + per_bank, chunk(c)], in_=result[:, t0 : t0 + per_bank, chunk(c)])

        def piece(c):
            return slice(OUT_STARTS[c], OUT_STARTS[c] + OUT_WIDTHS[c])

        def group_out(c):
            out_grouped[c] = keep.tile([P, OUT_WIDTHS[c], PACK], BF16, name="out_grouped%d" % c, align_bytes=MX_ALIGN)
            copy = nc.scalar.copy if c == PIECES - 1 else nc.vector.tensor_copy
            interleave(copy, out_grouped[c][:], result[:, :, piece(c)])

        def hand_on(c):
            step = P if OUT_STARTS[c] >= BANK else OUT_WIDTHS[c]
            for c0 in range(0, OUT_WIDTHS[c], step):
                strip, first = divmod(OUT_STARTS[c] + c0, STRIP)
                nc.vector.quantize_mx(
                    out=out_codes[:, OUT_STARTS[c] + c0 : OUT_STARTS[c] + c0 + step].bitcast(FP8X4),
                    scales=out_scales[4 * strip :, first : first + step],
                    in_=out_grouped[c][:, c0 : c0 + step, :].rearrange("p c t -> p (c t)"),
                )

        z_grouped[0] = first_grouped
        for t in range(PACK):
            quantize_w2(t)
        second_product(0)
        group_z(1)
        for c in range(1, CHUNKS - 1):
            group_z(c + 1)
            second_product(c)
        second_product(CHUNKS - 1)
        group_out(0)
        for c in range(PIECES - 1):
            group_out(c + 1)
            hand_on(c)
        hand_on(PIECES - 1)

        for cols in (slice(0, OUT_STARTS[3]), slice(OUT_STARTS[3], S)):
            nc.sync.dma_start(out=out_words[:, cols], in_=out_codes[:, cols])
        for q in range(QUADS):
            queue = nc.sync if q % 2 == 0 else nc.scalar
            queue.dma_start(
                out=out_2[0, 4 * q : 4 * q + 4, :].bitcast(I32).rearrange("r (j n) -> j r n", j=QUADS),
                in_=out_scales[32 * q : 32 * q + 16, :].bitcast(I32),
            )
